import numpy as np
import ml_dtypes


def mxq(x, axis, fmt="e4m3"):
    dtype, down = {"e4m3": (ml_dtypes.float8_e4m3fn, 7), "e5m2": (ml_dtypes.float8_e5m2, 14)}[fmt]
    v = np.moveaxis(np.asarray(x, np.float32).astype(ml_dtypes.bfloat16).astype(np.float64), axis, -1)
    blocks = v.reshape(v.shape[:-1] + (-1, 32))
    amax = np.abs(blocks).max(-1, keepdims=True)
    byte = np.maximum(np.where(amax > 0, np.frexp(amax)[1] - 1 + 127, 0) - down, 1)
    scale = np.exp2(byte - 127.0)
    codes = (blocks / scale).astype(np.float32).astype(dtype).astype(np.float64)
    return np.moveaxis((codes * scale).reshape(v.shape), -1, axis)


WIDE = False


def mx_kscale(k):
    if not WIDE:
        return np.ones(k)
    levels = np.array([10, -10, 5, -5, 0])
    if k % 512:
        return np.exp2(np.random.permutation(np.resize(levels, k // 32))).repeat(32)
    a = np.empty((k // 512, 16))
    for p in range(k // 512):
        a[p, :8] = np.random.permutation(np.resize(levels, 8))
        for g in range(8):
            far = levels[np.abs(levels - a[p, g]) >= 10]
            a[p, g + 8] = far[np.random.randint(len(far))]
    return np.exp2(a.ravel()).repeat(32)


def f64(x):
    return np.asarray(x).astype(np.float64)


def striped(idx):
    return np.tile(idx.reshape(-1, 16).T, (8, 1)).astype(np.uint16)


def unstriped(offs):
    return offs[:16].T.reshape(-1).astype(np.int64)


E2M1 = np.array([0.0, 0.5, 1.0, 1.5, 2.0, 3.0, 4.0, 6.0, -0.0, -0.5, -1.0, -1.5, -2.0, -3.0, -4.0, -6.0])


def pack_fp4(w):
    k, n = w.shape
    w = f64(np.asarray(w, np.float32).astype(ml_dtypes.bfloat16)).reshape(k // 32, 32, n)
    amax = np.abs(w).max(1)
    mant, ex = np.frexp(amax / 6.0)
    byte = np.clip(np.where(amax > 0, np.where(mant > 0.5, ex, ex - 1) + 127, 1), 1, 254)
    scaled = (w * np.exp2(127.0 - byte)[:, None, :]).reshape(k, n).astype(np.float32)
    c = np.ascontiguousarray(scaled.reshape(k // 512, 128, 4, n).transpose(0, 1, 3, 2)).astype(ml_dtypes.float4_e2m1fn).view(np.uint8) & 0xF
    words = (c[..., 0::2] | (c[..., 1::2] << 4)).reshape(k // 512, 128, 2 * n)
    return np.ascontiguousarray(words), np.ascontiguousarray(byte.astype(np.uint8).reshape(k // 512, 16, n))


def unpack_fp4(words, scales):
    g, _, n = scales.shape
    words = np.ascontiguousarray(words).reshape(g, 128, n, 2)
    nib = np.empty((g, 128, n, 4), np.uint8)
    nib[..., 0::2] = words & 0xF
    nib[..., 1::2] = words >> 4
    vals = E2M1[nib] * np.repeat(np.exp2(scales.astype(np.float64) - 127.0), 8, axis=1)[..., None]
    return vals.transpose(0, 1, 3, 2).reshape(g * 512, n)


def silu(v):
    return v / (1.0 + np.exp(-np.maximum(v, -700.0)))


K, T, S, H, N, U = 1024, 1024, 512, 512, 128, 1024
P = 2 ** 7


def setup_inputs():
    n = np.random.standard_normal
    s = mx_kscale(K)[:, None]
    u = mx_kscale(H)
    packed_w2 = pack_fp4(n((H, N)) / np.sqrt(H) / u[:, None])
    return {
        "xT": (n((K, T)) * s).astype(np.float32),
        "gate": np.tile(np.random.uniform(0.5, 1.5, S), (P, 1)).astype(np.float32),
        "w1": (n((K, H)) / np.sqrt(K) / s).astype(np.float32),
        "w3": (n((K, H)) / np.sqrt(K) / s * u).astype(np.float32),
        "w2_words": packed_w2[0],
        "w2_scales": packed_w2[1],
        "offs": striped(np.random.permutation(T)[:S]),
        "dst": striped(np.random.permutation(U)[:S]),
    }


def reference(xT, gate, w1, w3, w2_words, w2_scales, offs, dst):
    xq = mxq(f64(xT)[:, unstriped(offs)], 0, "e4m3")
    h = (silu(mxq(f64(w1), 0, "e4m3").T @ xq)) * ((mxq(f64(w3), 0, "e4m3").T @ xq))
    y = unpack_fp4(w2_words, w2_scales).T @ mxq(h, 0, "e4m3")
    out = np.zeros((N, U))
    out[:, unstriped(dst)] = y * f64(gate)[:1]
    return out

@@ -1,0 +1,211 @@
+from contextlib import ExitStack
+
+import concourse.mybir as mybir
+
+K, T, S, H, N, U = 1024, 1024, 512, 512, 128, 1024
+FLOPS = 2 * S * (2 * K * H + H * N)
+
+F32 = mybir.dt.float32
+BF16 = mybir.dt.bfloat16
+I32 = mybir.dt.int32
+U32 = mybir.dt.uint32
+U16 = mybir.dt.uint16
+U8 = mybir.dt.uint8
+FP8X4 = mybir.dt.float8_e4m3fn_x4
+FP4X4 = mybir.dt.float4_e2m1fn_x4
+ACT = mybir.ActivationFunctionType
+MULT = mybir.AluOpType.mult
+
+P = 128
+PACK = 4
+K_PASS = P * PACK
+PASSES = K // K_PASS
+X_COLS = 512
+W_COLS = 256
+M_HALF = W_COLS // PACK
+CHUNK = 128
+CHUNKS = S // CHUNK
+LIST_COLS = CHUNK // 16
+
+
+def tile_picked_route2_glusilu_e_kernel(tc, xT, gate, w1, w3, w2_words, w2_scales, offs, dst, out):
+    nc = tc.nc
+
+    with ExitStack() as ctx:
+        keep = ctx.enter_context(tc.tile_pool(name="keep", bufs=1))
+        psum = ctx.enter_context(tc.psum_pool(name="psum", bufs=8))
+
+        def rows_of(src, g):
+            return src[g * K_PASS : (g + 1) * K_PASS, :].rearrange("(p j) c -> p j c", j=PACK)
+
+        def load(src, g, c0, width, name):
+            raw = keep.tile([P, PACK, width], F32, name=name)
+            nc.sync.dma_start(out=raw[:], in_=rows_of(src, g)[:, :, c0 : c0 + width])
+            return raw
+
+        def cast(engine, dst_ap, src_ap):
+            if engine == "scalar":
+                nc.scalar.activation(dst_ap, src_ap, ACT.Copy)
+            else:
+                nc.vector.tensor_copy(dst_ap, src_ap)
+
+        window = keep.tile([P, U], F32, name="window")
+        nc.vector.memset(window[:], 0.0)
+        x_scales = keep.tile([P, T], U8, name="x_scales", align_bytes=64)
+        nc.gpsimd.memset(x_scales[:], 0)
+        w2_plane = keep.tile([P, N], U8, name="w2_plane", align_bytes=64)
+        nc.gpsimd.memset(w2_plane[:], 0)
+
+        x_raw = {}
+        x_raw[0, 0] = load(xT, 0, 0, X_COLS, "x_raw00")
+        offsets = keep.tile([P, S // 16], U16, name="offsets")
+        nc.sync.dma_start(offsets[:], offs)
+        for g, half in ((0, 1), (1, 0), (1, 1)):
+            x_raw[g, half] = load(xT, g, half * X_COLS, X_COLS, "x_raw%d%d" % (g, half))
+        w_raw = {}
+        for mat, g in ((0, 0), (0, 1), (1, 0)):
+            whole = load((w1, w3)[mat], g, 0, H, "w_raw%d%d" % (mat, g))
+            for half in range(2):
+                w_raw[mat, g, half] = whole[:, :, half * W_COLS : (half + 1) * W_COLS]
+        for half in range(2):
+            w_raw[1, 1, half] = load(w3, 1, half * W_COLS, W_COLS, "w_last%d" % half)[:]
+        w2_codes = keep.tile([P, 2 * N], U8, name="w2_codes", align_bytes=64)
+        nc.sync.dma_start(w2_codes[:].bitcast(I32), w2_words[0].bitcast(I32))
+        for q in range(4):
+            nc.sync.dma_start(
+                w2_plane[32 * q : 32 * q + 4, :].bitcast(I32), w2_scales[0, 4 * q : 4 * q + 4, :].bitcast(I32)
+            )
+        places = keep.tile([P, S // 16], U16, name="places")
+        nc.sync.dma_start(places[:], dst)
+        gates = keep.tile([P, S], F32, name="gates")
+        nc.sync.dma_start(gates[:], gate)
+
+        x_words = [keep.tile([P, T], U32, name="x_words%d" % g, align_bytes=64) for g in range(PASSES)]
+        picked_words = [keep.tile([P, S], U32, name="picked_words%d" % g, align_bytes=64) for g in range(PASSES)]
+        picked_scales = keep.tile([P, S], U8, name="picked_scales", align_bytes=64)
+
+        def quantise_tokens(g, half, scalar_cols):
+            rounded = keep.tile([P, X_COLS, PACK], BF16, name="x_bf%d%d" % (g, half), align_bytes=64)
+            for engine, c0, c1 in (("scalar", 0, scalar_cols), ("vector", scalar_cols, X_COLS)):
+                if c1 > c0:
+                    cast(
+                        engine,
+                        rounded[:, c0:c1, :].rearrange("p (c i) j -> p c j i", i=4),
+                        x_raw[g, half][:, :, c0:c1].rearrange("p j (c i) -> p c j i", i=4),
+                    )
+            cols = slice(half * X_COLS, (half + 1) * X_COLS)
+            nc.vector.quantize_mx(
+                out=x_words[g][:, cols].bitcast(FP8X4),
+                scales=x_scales[4 * g : P, cols],
+                in_=rounded[:].rearrange("p c j -> p (c j)"),
+            )
+
+        def pick(picked, table):
+            nc.vector.tensor_copy(picked[:], table[:].indirect(offsets[:]))
+
+        quantise_tokens(0, 0, 512)
+        quantise_tokens(0, 1, 512)
+        pick(picked_words[0], x_words[0])
+        quantise_tokens(1, 0, 512)
+        quantise_tokens(1, 1, 176)
+        pick(picked_scales, x_scales)
+        pick(picked_words[1], x_words[1])
+
+        w_words, w_scales = {}, {}
+
+        def quantise_weights(mat, g, engines):
+            words = keep.tile([P, H], U32, name="w_words%d%d" % (mat, g), align_bytes=64)
+            scales = keep.tile([P, H], U8, name="w_scales%d%d" % (mat, g), align_bytes=64)
+            w_words[mat, g], w_scales[mat, g] = words, scales
+            for half in range(2):
+                rounded = keep.tile([P, PACK, M_HALF, PACK], BF16, name="w_bf%d%d%d" % (mat, g, half), align_bytes=64)
+                cast(
+                    engines[half],
+                    rounded[:].rearrange("p t m j -> p m j t"),
+                    w_raw[mat, g, half].rearrange("p j (m t) -> p m j t", t=PACK),
+                )
+                for t in range(PACK):
+                    cols = slice(t * P + half * M_HALF, t * P + (half + 1) * M_HALF)
+                    nc.vector.quantize_mx(
+                        out=words[:, cols].bitcast(FP8X4),
+                        scales=scales[:, cols],
+                        in_=rounded[:, t, :, :].rearrange("p m j -> p (m j)"),
+                    )
+
+        def first_layer_pass(acc, mat, g, t, tokens):
+            cols = slice(t * P, (t + 1) * P)
+            nc.tensor.matmul_mx(
+                out=acc,
+                lhsT=w_words[mat, g][:, cols].bitcast(FP8X4),
+                lhsT_scale=w_scales[mat, g][:, cols],
+                rhs=picked_words[g][:, tokens].bitcast(FP8X4),
+                rhs_scale=picked_scales[4 * g : P, tokens],
+                start=(g == 0),
+                stop=(g == PASSES - 1),
+            )
+
+        a_banks = [psum.tile([P, S], F32, name="a_bank%d" % t, tag="bank") for t in range(PACK)]
+        quantise_weights(0, 0, ("scalar", "scalar"))
+        for t in range(PACK):
+            first_layer_pass(a_banks[t][:], 0, 0, t, slice(0, S))
+        quantise_weights(0, 1, ("scalar", "vector"))
+        for t in range(PACK):
+            first_layer_pass(a_banks[t][:], 0, 1, t, slice(0, S))
+        quantise_weights(1, 0, ("scalar", "vector"))
+        silu_a = keep.tile([P, PACK, S], F32, name="silu_a")
+        for t in range(PACK):
+            nc.scalar.activation(silu_a[:, t, :], a_banks[t][:], ACT.Silu)
+        quantise_weights(1, 1, ("vector", "vector"))
+
+        hidden, results = {}, {}
+
+        def gated_product(c):
+            tokens = slice(c * CHUNK, (c + 1) * CHUNK)
+            b_bank = psum.tile([P, PACK, CHUNK], F32, name="b_bank%d" % c, tag="bank")
+            for t in range(PACK):
+                for g in range(PASSES):
+                    first_layer_pass(b_bank[:, t, :], 1, g, t, tokens)
+            hidden[c] = keep.tile([P, CHUNK, PACK], BF16, name="hidden%d" % c, align_bytes=64)
+            nc.vector.tensor_tensor(
+                hidden[c][:].rearrange("p (c i) t -> p c t i", i=4),
+                b_bank[:].rearrange("p t (c i) -> p c t i", i=4),
+                silu_a[:, :, tokens].rearrange("p t (c i) -> p c t i", i=4),
+                MULT,
+            )
+
+        def second_layer(c):
+            words = keep.tile([P, CHUNK], U32, name="h_words%d" % c, align_bytes=64)
+            scales = keep.tile([P, CHUNK], U8, name="h_scales%d" % c, align_bytes=64)
+            nc.vector.quantize_mx(
+                out=words[:].bitcast(FP8X4), scales=scales[:], in_=hidden[c][:].rearrange("p c t -> p (c t)")
+            )
+            y_bank = psum.tile([P, CHUNK], F32, name="y_bank%d" % c, tag="bank")
+            nc.tensor.matmul_mx(
+                out=y_bank[:],
+                lhsT=w2_codes[:].bitcast(FP4X4),
+                lhsT_scale=w2_plane[:],
+                rhs=words[:].bitcast(FP8X4),
+                rhs_scale=scales[:],
+                start=True,
+                stop=True,
+            )
+            results[c] = keep.tile([P, CHUNK], F32, name="result%d" % c)
+            nc.scalar.activation(results[c][:], y_bank[:], ACT.Copy)
+
+        def put(c):
+            nc.vector.tensor_tensor(
+                window[:].indirect(places[:, c * LIST_COLS : (c + 1) * LIST_COLS]),
+                results[c][:],
+                gates[:, c * CHUNK : (c + 1) * CHUNK],
+                MULT,
+            )
+
+        for step in range(CHUNKS + 3):
+            if step < CHUNKS:
+                gated_product(step)
+            if step >= 3:
+                put(step - 3)
+            if 1 <= step <= CHUNKS:
+                second_layer(step - 1)
+
+        nc.sync.dma_start(out, window[:])

@@ -22,7 +22,6 @@ K_PASS = P * PACK
 PASSES = K // K_PASS
 X_COLS = 512
 W_COLS = 256
-M_HALF = W_COLS // PACK
 CHUNK = 128
 CHUNKS = S // CHUNK
 LIST_COLS = CHUNK // 16
@@ -33,13 +32,13 @@ def tile_picked_route2_glusilu_e_kernel(tc, xT, gate, w1, w3, w2_words, w2_scale
 
     with ExitStack() as ctx:
         keep = ctx.enter_context(tc.tile_pool(name="keep", bufs=1))
-        psum = ctx.enter_context(tc.psum_pool(name="psum", bufs=8))
+        psum = ctx.enter_context(tc.psum_pool(name="psum", bufs=1))
 
         def rows_of(src, g):
             return src[g * K_PASS : (g + 1) * K_PASS, :].rearrange("(p j) c -> p j c", j=PACK)
 
         def load(src, g, c0, width, name):
-            raw = keep.tile([P, PACK, width], F32, name=name)
+            raw = keep.tile([P, PACK, width], F32, name=name, tag=name)
             nc.sync.dma_start(out=raw[:], in_=rows_of(src, g)[:, :, c0 : c0 + width])
             return raw
 
@@ -52,9 +51,12 @@ def tile_picked_route2_glusilu_e_kernel(tc, xT, gate, w1, w3, w2_words, w2_scale
         window = keep.tile([P, U], F32, name="window")
         nc.vector.memset(window[:], 0.0)
         x_scales = keep.tile([P, T], U8, name="x_scales", align_bytes=64)
-        nc.gpsimd.memset(x_scales[:], 0)
+        nc.vector.memset(x_scales[:].bitcast(I32), 0)
         w2_plane = keep.tile([P, N], U8, name="w2_plane", align_bytes=64)
-        nc.gpsimd.memset(w2_plane[:], 0)
+        nc.vector.memset(w2_plane[:].bitcast(I32), 0)
+
+        warm = keep.tile([P, 8], F32, name="warm")
+        nc.scalar.activation(warm[:], window[:, 0:8], ACT.Silu)
 
         x_raw = {}
         x_raw[0, 0] = load(xT, 0, 0, X_COLS, "x_raw00")
@@ -64,11 +66,8 @@ def tile_picked_route2_glusilu_e_kernel(tc, xT, gate, w1, w3, w2_words, w2_scale
             x_raw[g, half] = load(xT, g, half * X_COLS, X_COLS, "x_raw%d%d" % (g, half))
         w_raw = {}
         for mat, g in ((0, 0), (0, 1), (1, 0)):
-            whole = load((w1, w3)[mat], g, 0, H, "w_raw%d%d" % (mat, g))
-            for half in range(2):
-                w_raw[mat, g, half] = whole[:, :, half * W_COLS : (half + 1) * W_COLS]
-        for half in range(2):
-            w_raw[1, 1, half] = load(w3, 1, half * W_COLS, W_COLS, "w_last%d" % half)[:]
+            w_raw[mat, g] = [load((w1, w3)[mat], g, 0, H, "w_raw%d%d" % (mat, g))]
+        w_raw[1, 1] = [load(w3, 1, half * W_COLS, W_COLS, "w_last%d" % half) for half in range(2)]
         w2_codes = keep.tile([P, 2 * N], U8, name="w2_codes", align_bytes=64)
         nc.sync.dma_start(w2_codes[:].bitcast(I32), w2_words[0].bitcast(I32))
         for q in range(4):
@@ -103,10 +102,10 @@ def tile_picked_route2_glusilu_e_kernel(tc, xT, gate, w1, w3, w2_words, w2_scale
         def pick(picked, table):
             nc.vector.tensor_copy(picked[:], table[:].indirect(offsets[:]))
 
-        quantise_tokens(0, 0, 512)
-        quantise_tokens(0, 1, 512)
+        quantise_tokens(0, 0, 320)
+        quantise_tokens(0, 1, 320)
         pick(picked_words[0], x_words[0])
-        quantise_tokens(1, 0, 512)
+        quantise_tokens(1, 0, 320)
         quantise_tokens(1, 1, 176)
         pick(picked_scales, x_scales)
         pick(picked_words[1], x_words[1])
@@ -117,20 +116,32 @@ def tile_picked_route2_glusilu_e_kernel(tc, xT, gate, w1, w3, w2_words, w2_scale
             words = keep.tile([P, H], U32, name="w_words%d%d" % (mat, g), align_bytes=64)
             scales = keep.tile([P, H], U8, name="w_scales%d%d" % (mat, g), align_bytes=64)
             w_words[mat, g], w_scales[mat, g] = words, scales
-            for half in range(2):
-                rounded = keep.tile([P, PACK, M_HALF, PACK], BF16, name="w_bf%d%d%d" % (mat, g, half), align_bytes=64)
-                cast(
-                    engines[half],
-                    rounded[:].rearrange("p t m j -> p m j t"),
-                    w_raw[mat, g, half].rearrange("p j (m t) -> p m j t", t=PACK),
-                )
-                for t in range(PACK):
-                    cols = slice(t * P + half * M_HALF, t * P + (half + 1) * M_HALF)
-                    nc.vector.quantize_mx(
-                        out=words[:, cols].bitcast(FP8X4),
-                        scales=scales[:, cols],
-                        in_=rounded[:, t, :, :].rearrange("p m j -> p (m j)"),
+            pieces = w_raw[mat, g]
+            m_cols = P // len(pieces)
+            for piece, raw in enumerate(pieces):
+                rounded = {}
+                for pair in range(2):
+                    rounded[pair] = keep.tile(
+                        [P, 2, m_cols, PACK], BF16, name="w_bf%d%d%d%d" % (mat, g, piece, pair), align_bytes=64
                     )
+                    cast(
+                        engines[pair],
+                        rounded[pair][:].rearrange("p t m j -> p m j t"),
+                        raw[:].rearrange("p j (m t) -> p m j t", t=PACK)[:, :, :, 2 * pair : 2 * pair + 2],
+                    )
+                for pair in range(2):
+                    if m_cols == P:
+                        calls = [(slice(2 * pair * P, (2 * pair + 2) * P), rounded[pair][:].rearrange("p t m j -> p (t m j)"))]
+                    else:
+                        calls = [
+                            (
+                                slice((2 * pair + u) * P + piece * m_cols, (2 * pair + u) * P + (piece + 1) * m_cols),
+                                rounded[pair][:, u, :, :].rearrange("p m j -> p (m j)"),
+                            )
+                            for u in range(2)
+                        ]
+                    for cols, values in calls:
+                        nc.vector.quantize_mx(out=words[:, cols].bitcast(FP8X4), scales=scales[:, cols], in_=values)
 
         def first_layer_pass(acc, mat, g, t, tokens):
             cols = slice(t * P, (t + 1) * P)
@@ -144,42 +155,49 @@ def tile_picked_route2_glusilu_e_kernel(tc, xT, gate, w1, w3, w2_words, w2_scale
                 stop=(g == PASSES - 1),
             )
 
-        a_banks = [psum.tile([P, S], F32, name="a_bank%d" % t, tag="bank") for t in range(PACK)]
-        quantise_weights(0, 0, ("scalar", "scalar"))
-        for t in range(PACK):
-            first_layer_pass(a_banks[t][:], 0, 0, t, slice(0, S))
-        quantise_weights(0, 1, ("scalar", "vector"))
-        for t in range(PACK):
-            first_layer_pass(a_banks[t][:], 0, 1, t, slice(0, S))
-        quantise_weights(1, 0, ("scalar", "vector"))
-        silu_a = keep.tile([P, PACK, S], F32, name="silu_a")
-        for t in range(PACK):
-            nc.scalar.activation(silu_a[:, t, :], a_banks[t][:], ACT.Silu)
-        quantise_weights(1, 1, ("vector", "vector"))
-
-        hidden, results = {}, {}
-
-        def gated_product(c):
-            tokens = slice(c * CHUNK, (c + 1) * CHUNK)
-            b_bank = psum.tile([P, PACK, CHUNK], F32, name="b_bank%d" % c, tag="bank")
+        def first_layer(mat, c):
+            bank = psum.tile([P, PACK, CHUNK], F32, name="bank%d%d" % (mat, c), tag="bank%d%d" % (mat, c))
             for t in range(PACK):
                 for g in range(PASSES):
-                    first_layer_pass(b_bank[:, t, :], 1, g, t, tokens)
+                    first_layer_pass(bank[:, t, :], mat, g, t, slice(c * CHUNK, (c + 1) * CHUNK))
+            return bank
+
+        quantise_weights(0, 0, ("scalar", "scalar"))
+        quantise_weights(0, 1, ("vector", "scalar"))
+        a_banks = [first_layer(0, c) for c in range(CHUNKS)]
+        quantise_weights(1, 0, ("vector", "scalar"))
+        quantise_weights(1, 1, ("vector", "scalar"))
+        silu_a = keep.tile([P, CHUNKS, CHUNK, PACK], F32, name="silu_a", tag="w_last1")
+        for c in range(CHUNKS):
+            nc.scalar.activation(silu_a[:, c, :, :], a_banks[c][:].rearrange("p t c -> p c t"), ACT.Silu)
+
+        b_banks = [first_layer(1, c) for c in range(CHUNKS)]
+        hidden = {}
+        results = keep.tile([P, S], F32, name="results")
+
+        def gated_product(c):
+            b_bank = b_banks[c]
             hidden[c] = keep.tile([P, CHUNK, PACK], BF16, name="hidden%d" % c, align_bytes=64)
             nc.vector.tensor_tensor(
-                hidden[c][:].rearrange("p (c i) t -> p c t i", i=4),
-                b_bank[:].rearrange("p t (c i) -> p c t i", i=4),
-                silu_a[:, :, tokens].rearrange("p t (c i) -> p c t i", i=4),
+                hidden[c][:],
+                b_bank[:].rearrange("p t c -> p c t"),
+                silu_a[:, c, :, :],
                 MULT,
             )
 
-        def second_layer(c):
+        h_codes = {}
+
+        def quantise_hidden(c):
             words = keep.tile([P, CHUNK], U32, name="h_words%d" % c, align_bytes=64)
             scales = keep.tile([P, CHUNK], U8, name="h_scales%d" % c, align_bytes=64)
             nc.vector.quantize_mx(
                 out=words[:].bitcast(FP8X4), scales=scales[:], in_=hidden[c][:].rearrange("p c t -> p (c t)")
             )
-            y_bank = psum.tile([P, CHUNK], F32, name="y_bank%d" % c, tag="bank")
+            h_codes[c] = words, scales
+
+        def second_layer(c):
+            words, scales = h_codes[c]
+            y_bank = psum.tile([P, CHUNK], F32, name="y_bank%d" % c, tag=("bank12", "bank13", "bank00", "bank01")[c])
             nc.tensor.matmul_mx(
                 out=y_bank[:],
                 lhsT=w2_codes[:].bitcast(FP4X4),
@@ -189,23 +207,29 @@ def tile_picked_route2_glusilu_e_kernel(tc, xT, gate, w1, w3, w2_words, w2_scale
                 start=True,
                 stop=True,
             )
-            results[c] = keep.tile([P, CHUNK], F32, name="result%d" % c)
-            nc.scalar.activation(results[c][:], y_bank[:], ACT.Copy)
+            nc.scalar.activation(results[:, c * CHUNK : (c + 1) * CHUNK], y_bank[:], ACT.Copy)
 
-        def put(c):
+        def put(c0, c1):
             nc.vector.tensor_tensor(
-                window[:].indirect(places[:, c * LIST_COLS : (c + 1) * LIST_COLS]),
-                results[c][:],
-                gates[:, c * CHUNK : (c + 1) * CHUNK],
+                window[:].indirect(places[:, c0 * LIST_COLS : c1 * LIST_COLS]),
+                results[:, c0 * CHUNK : c1 * CHUNK],
+                gates[:, c0 * CHUNK : c1 * CHUNK],
                 MULT,
             )
 
-        for step in range(CHUNKS + 3):
-            if step < CHUNKS:
-                gated_product(step)
-            if step >= 3:
-                put(step - 3)
-            if 1 <= step <= CHUNKS:
-                second_layer(step - 1)
+        gated_product(0)
+        gated_product(1)
+        quantise_hidden(0)
+        gated_product(2)
+        second_layer(0)
+        quantise_hidden(1)
+        gated_product(3)
+        second_layer(1)
+        quantise_hidden(2)
+        second_layer(2)
+        put(0, 1)
+        quantise_hidden(3)
+        second_layer(3)
+        put(1, CHUNKS)
 
         nc.sync.dma_start(out, window[:])

@@ -20,11 +20,18 @@ P = 128
 PACK = 4
 K_PASS = P * PACK
 PASSES = K // K_PASS
-X_COLS = 512
-W_COLS = 256
+LIST_ROWS = 16
+SCALE_ROWS = 4
+LINE = 4
+W1, W3 = 0, 1
+
+X_COLS = T // 2
+SCALAR_COLS = 320
+SCALAR_COLS_LAST = 176
+
 CHUNK = 128
 CHUNKS = S // CHUNK
-LIST_COLS = CHUNK // 16
+LIST_COLS = CHUNK // LIST_ROWS
 
 
 def tile_picked_route2_glusilu_e_kernel(tc, xT, gate, w1, w3, w2_words, w2_scales, offs, dst, out):
@@ -34,19 +41,17 @@ def tile_picked_route2_glusilu_e_kernel(tc, xT, gate, w1, w3, w2_words, w2_scale
         keep = ctx.enter_context(tc.tile_pool(name="keep", bufs=1))
         psum = ctx.enter_context(tc.psum_pool(name="psum", bufs=1))
 
-        def rows_of(src, g):
-            return src[g * K_PASS : (g + 1) * K_PASS, :].rearrange("(p j) c -> p j c", j=PACK)
-
-        def load(src, g, c0, width, name):
+        def load(src, g, first, width, name):
             raw = keep.tile([P, PACK, width], F32, name=name, tag=name)
-            nc.sync.dma_start(out=raw[:], in_=rows_of(src, g)[:, :, c0 : c0 + width])
+            rows = src[g * K_PASS : (g + 1) * K_PASS, :].rearrange("(p j) c -> p j c", j=PACK)
+            nc.sync.dma_start(out=raw[:], in_=rows[:, :, first : first + width])
             return raw
 
-        def cast(engine, dst_ap, src_ap):
-            if engine == "scalar":
-                nc.scalar.activation(dst_ap, src_ap, ACT.Copy)
-            else:
-                nc.vector.tensor_copy(dst_ap, src_ap)
+        def round_on_scalar(rounded, raw):
+            nc.scalar.activation(rounded, raw, ACT.Copy)
+
+        def round_on_vector(rounded, raw):
+            nc.vector.tensor_copy(rounded, raw)
 
         window = keep.tile([P, U], F32, name="window")
         nc.vector.memset(window[:], 0.0)
@@ -58,23 +63,23 @@ def tile_picked_route2_glusilu_e_kernel(tc, xT, gate, w1, w3, w2_words, w2_scale
         warm = keep.tile([P, 8], F32, name="warm")
         nc.scalar.activation(warm[:], window[:, 0:8], ACT.Silu)
 
-        x_raw = {}
-        x_raw[0, 0] = load(xT, 0, 0, X_COLS, "x_raw00")
-        offsets = keep.tile([P, S // 16], U16, name="offsets")
+        x_raw = {(0, 0): load(xT, 0, 0, X_COLS, "x_raw00")}
+        offsets = keep.tile([P, S // LIST_ROWS], U16, name="offsets")
         nc.sync.dma_start(offsets[:], offs)
         for g, half in ((0, 1), (1, 0), (1, 1)):
             x_raw[g, half] = load(xT, g, half * X_COLS, X_COLS, "x_raw%d%d" % (g, half))
         w_raw = {}
-        for mat, g in ((0, 0), (0, 1), (1, 0)):
+        for mat, g in ((W1, 0), (W1, 1), (W3, 0)):
             w_raw[mat, g] = [load((w1, w3)[mat], g, 0, H, "w_raw%d%d" % (mat, g))]
-        w_raw[1, 1] = [load(w3, 1, half * W_COLS, W_COLS, "w_last%d" % half) for half in range(2)]
+        w_raw[W3, 1] = [load(w3, 1, half * H // 2, H // 2, "w_last%d" % half) for half in range(2)]
         w2_codes = keep.tile([P, 2 * N], U8, name="w2_codes", align_bytes=64)
         nc.sync.dma_start(w2_codes[:].bitcast(I32), w2_words[0].bitcast(I32))
-        for q in range(4):
+        for q in range(P // 32):
             nc.sync.dma_start(
-                w2_plane[32 * q : 32 * q + 4, :].bitcast(I32), w2_scales[0, 4 * q : 4 * q + 4, :].bitcast(I32)
+                w2_plane[32 * q : 32 * q + SCALE_ROWS, :].bitcast(I32),
+                w2_scales[0, SCALE_ROWS * q : SCALE_ROWS * (q + 1), :].bitcast(I32),
             )
-        places = keep.tile([P, S // 16], U16, name="places")
+        places = keep.tile([P, S // LIST_ROWS], U16, name="places")
         nc.sync.dma_start(places[:], dst)
         gates = keep.tile([P, S], F32, name="gates")
         nc.sync.dma_start(gates[:], gate)
@@ -85,34 +90,32 @@ def tile_picked_route2_glusilu_e_kernel(tc, xT, gate, w1, w3, w2_words, w2_scale
 
         def quantise_tokens(g, half, scalar_cols):
             rounded = keep.tile([P, X_COLS, PACK], BF16, name="x_bf%d%d" % (g, half), align_bytes=64)
-            for engine, c0, c1 in (("scalar", 0, scalar_cols), ("vector", scalar_cols, X_COLS)):
-                if c1 > c0:
-                    cast(
-                        engine,
-                        rounded[:, c0:c1, :].rearrange("p (c i) j -> p c j i", i=4),
-                        x_raw[g, half][:, :, c0:c1].rearrange("p j (c i) -> p c j i", i=4),
-                    )
+            for round_on, c0, c1 in ((round_on_scalar, 0, scalar_cols), (round_on_vector, scalar_cols, X_COLS)):
+                round_on(
+                    rounded[:, c0:c1, :].rearrange("p (c i) j -> p c j i", i=LINE),
+                    x_raw[g, half][:, :, c0:c1].rearrange("p j (c i) -> p c j i", i=LINE),
+                )
             cols = slice(half * X_COLS, (half + 1) * X_COLS)
             nc.vector.quantize_mx(
                 out=x_words[g][:, cols].bitcast(FP8X4),
-                scales=x_scales[4 * g : P, cols],
+                scales=x_scales[SCALE_ROWS * g : P, cols],
                 in_=rounded[:].rearrange("p c j -> p (c j)"),
             )
 
         def pick(picked, table):
             nc.vector.tensor_copy(picked[:], table[:].indirect(offsets[:]))
 
-        quantise_tokens(0, 0, 320)
-        quantise_tokens(0, 1, 320)
+        quantise_tokens(0, 0, SCALAR_COLS)
+        quantise_tokens(0, 1, SCALAR_COLS)
         pick(picked_words[0], x_words[0])
-        quantise_tokens(1, 0, 320)
-        quantise_tokens(1, 1, 176)
+        quantise_tokens(1, 0, SCALAR_COLS)
+        quantise_tokens(1, 1, SCALAR_COLS_LAST)
         pick(picked_scales, x_scales)
         pick(picked_words[1], x_words[1])
 
         w_words, w_scales = {}, {}
 
-        def quantise_weights(mat, g, engines):
+        def quantise_weights(mat, g, round_low, round_high):
             words = keep.tile([P, H], U32, name="w_words%d%d" % (mat, g), align_bytes=64)
             scales = keep.tile([P, H], U8, name="w_scales%d%d" % (mat, g), align_bytes=64)
             w_words[mat, g], w_scales[mat, g] = words, scales
@@ -120,27 +123,28 @@ def tile_picked_route2_glusilu_e_kernel(tc, xT, gate, w1, w3, w2_words, w2_scale
             m_cols = P // len(pieces)
             for piece, raw in enumerate(pieces):
                 rounded = {}
-                for pair in range(2):
+                for pair, round_on in enumerate((round_low, round_high)):
                     rounded[pair] = keep.tile(
                         [P, 2, m_cols, PACK], BF16, name="w_bf%d%d%d%d" % (mat, g, piece, pair), align_bytes=64
                     )
-                    cast(
-                        engines[pair],
-                        rounded[pair][:].rearrange("p t m j -> p m j t"),
+                    round_on(
+                        rounded[pair][:].rearrange("p u m j -> p m j u"),
                         raw[:].rearrange("p j (m t) -> p m j t", t=PACK)[:, :, :, 2 * pair : 2 * pair + 2],
                     )
                 for pair in range(2):
                     if m_cols == P:
-                        calls = [(slice(2 * pair * P, (2 * pair + 2) * P), rounded[pair][:].rearrange("p t m j -> p (t m j)"))]
+                        runs = [(2 * pair * P, 2 * P, rounded[pair][:].rearrange("p u m j -> p (u m j)"))]
                     else:
-                        calls = [
+                        runs = [
                             (
-                                slice((2 * pair + u) * P + piece * m_cols, (2 * pair + u) * P + (piece + 1) * m_cols),
+                                (2 * pair + u) * P + piece * m_cols,
+                                m_cols,
                                 rounded[pair][:, u, :, :].rearrange("p m j -> p (m j)"),
                             )
                             for u in range(2)
                         ]
-                    for cols, values in calls:
+                    for first, width, values in runs:
+                        cols = slice(first, first + width)
                         nc.vector.quantize_mx(out=words[:, cols].bitcast(FP8X4), scales=scales[:, cols], in_=values)
 
         def first_layer_pass(acc, mat, g, t, tokens):
@@ -150,42 +154,64 @@ def tile_picked_route2_glusilu_e_kernel(tc, xT, gate, w1, w3, w2_words, w2_scale
                 lhsT=w_words[mat, g][:, cols].bitcast(FP8X4),
                 lhsT_scale=w_scales[mat, g][:, cols],
                 rhs=picked_words[g][:, tokens].bitcast(FP8X4),
-                rhs_scale=picked_scales[4 * g : P, tokens],
+                rhs_scale=picked_scales[SCALE_ROWS * g : P, tokens],
                 start=(g == 0),
                 stop=(g == PASSES - 1),
             )
 
-        def first_layer(mat, c):
-            bank = psum.tile([P, PACK, CHUNK], F32, name="bank%d%d" % (mat, c), tag="bank%d%d" % (mat, c))
-            for t in range(PACK):
-                for g in range(PASSES):
-                    first_layer_pass(bank[:, t, :], mat, g, t, slice(c * CHUNK, (c + 1) * CHUNK))
-            return bank
+        quantise_weights(W1, 0, round_on_scalar, round_on_scalar)
+        w1_banks = {}
+        for half in range(2):
+            for pair in range(2):
+                name = "w1_bank%d" % (2 * half + pair)
+                w1_banks[half, pair] = psum.tile([P, 2, S // 2], F32, name=name, tag=name)
 
-        quantise_weights(0, 0, ("scalar", "scalar"))
-        quantise_weights(0, 1, ("vector", "scalar"))
-        a_banks = [first_layer(0, c) for c in range(CHUNKS)]
-        quantise_weights(1, 0, ("vector", "scalar"))
-        quantise_weights(1, 1, ("vector", "scalar"))
-        silu_a = keep.tile([P, CHUNKS, CHUNK, PACK], F32, name="silu_a", tag="w_last1")
+        def w1_pass(half, pair, u, g):
+            tokens = slice(half * S // 2, (half + 1) * S // 2)
+            first_layer_pass(w1_banks[half, pair][:, u, :], W1, g, 2 * pair + u, tokens)
+
+        for pair in range(2):
+            for half in range(2):
+                w1_pass(half, pair, 0, 0)
+        quantise_weights(W1, 1, round_on_vector, round_on_scalar)
+        for half in range(2):
+            for pair in range(2):
+                for u, g in ((0, 1), (1, 0), (1, 1)):
+                    w1_pass(half, pair, u, g)
+
+        quantise_weights(W3, 0, round_on_vector, round_on_scalar)
+        quantise_weights(W3, 1, round_on_vector, round_on_scalar)
+
+        silu_w1 = keep.tile([P, CHUNKS, 2, CHUNK, 2], F32, name="silu_w1", tag="w_last1")
         for c in range(CHUNKS):
-            nc.scalar.activation(silu_a[:, c, :, :], a_banks[c][:].rearrange("p t c -> p c t"), ACT.Silu)
+            for pair in range(2):
+                sums = w1_banks[c // 2, pair][:, :, (c % 2) * CHUNK : (c % 2 + 1) * CHUNK]
+                nc.scalar.activation(silu_w1[:, c, pair, :, :], sums.rearrange("p u c -> p c u"), ACT.Silu)
 
-        b_banks = [first_layer(1, c) for c in range(CHUNKS)]
-        hidden = {}
+        w3_banks = [psum.tile([P, PACK, CHUNK], F32, name="w3_bank%d" % c, tag="w3_bank%d" % c) for c in range(CHUNKS)]
+
+        def w3_pass(c, t, g):
+            first_layer_pass(w3_banks[c][:, t, :], W3, g, t, slice(c * CHUNK, (c + 1) * CHUNK))
+
+        for c in range(CHUNKS):
+            w3_pass(c, 0, 0)
+        for c in range(CHUNKS):
+            w3_pass(c, 0, 1)
+            for t in range(1, PACK):
+                for g in range(PASSES):
+                    w3_pass(c, t, g)
+
+        hidden, h_codes = {}, {}
         results = keep.tile([P, S], F32, name="results")
 
         def gated_product(c):
-            b_bank = b_banks[c]
             hidden[c] = keep.tile([P, CHUNK, PACK], BF16, name="hidden%d" % c, align_bytes=64)
             nc.vector.tensor_tensor(
-                hidden[c][:],
-                b_bank[:].rearrange("p t c -> p c t"),
-                silu_a[:, c, :, :],
+                hidden[c][:].rearrange("p c (r u) -> p c r u", u=2),
+                w3_banks[c][:].rearrange("p (r u) c -> p c r u", u=2),
+                silu_w1[:, c, :, :, :].rearrange("p r c u -> p c r u"),
                 MULT,
             )
-
-        h_codes = {}
 
         def quantise_hidden(c):
             words = keep.tile([P, CHUNK], U32, name="h_words%d" % c, align_bytes=64)
@@ -195,9 +221,11 @@ def tile_picked_route2_glusilu_e_kernel(tc, xT, gate, w1, w3, w2_words, w2_scale
             )
             h_codes[c] = words, scales
 
+        y_tags = ("w3_bank2", "w3_bank3", "w1_bank0", "w1_bank1")
+
         def second_layer(c):
             words, scales = h_codes[c]
-            y_bank = psum.tile([P, CHUNK], F32, name="y_bank%d" % c, tag=("bank12", "bank13", "bank00", "bank01")[c])
+            y_bank = psum.tile([P, CHUNK], F32, name="y_bank%d" % c, tag=y_tags[c])
             nc.tensor.matmul_mx(
                 out=y_bank[:],
                 lhsT=w2_codes[:].bitcast(FP4X4),

@@ -26,8 +26,7 @@ LINE = 4
 W1, W3 = 0, 1
 
 X_COLS = T // 2
-SCALAR_COLS = 320
-SCALAR_COLS_LAST = 176
+SCALAR_COLS = 448
 
 CHUNK = 128
 CHUNKS = S // CHUNK
@@ -63,11 +62,10 @@ def tile_picked_route2_glusilu_e_kernel(tc, xT, gate, w1, w3, w2_words, w2_scale
         warm = keep.tile([P, 8], F32, name="warm")
         nc.scalar.activation(warm[:], window[:, 0:8], ACT.Silu)
 
-        x_raw = {(0, 0): load(xT, 0, 0, X_COLS, "x_raw00")}
+        x_raw = {0: load(xT, 0, 0, T, "x_raw0")}
         offsets = keep.tile([P, S // LIST_ROWS], U16, name="offsets")
         nc.sync.dma_start(offsets[:], offs)
-        for g, half in ((0, 1), (1, 0), (1, 1)):
-            x_raw[g, half] = load(xT, g, half * X_COLS, X_COLS, "x_raw%d%d" % (g, half))
+        x_raw[1] = load(xT, 1, 0, T, "x_raw1")
         w_raw = {}
         for mat, g in ((W1, 0), (W1, 1), (W3, 0)):
             w_raw[mat, g] = [load((w1, w3)[mat], g, 0, H, "w_raw%d%d" % (mat, g))]
@@ -88,28 +86,32 @@ def tile_picked_route2_glusilu_e_kernel(tc, xT, gate, w1, w3, w2_words, w2_scale
         picked_words = [keep.tile([P, S], U32, name="picked_words%d" % g, align_bytes=64) for g in range(PASSES)]
         picked_scales = keep.tile([P, S], U8, name="picked_scales", align_bytes=64)
 
-        def quantise_tokens(g, half, scalar_cols):
-            rounded = keep.tile([P, X_COLS, PACK], BF16, name="x_bf%d%d" % (g, half), align_bytes=64)
-            for round_on, c0, c1 in ((round_on_scalar, 0, scalar_cols), (round_on_vector, scalar_cols, X_COLS)):
+        def quantise_tokens(g):
+            rounded = keep.tile([P, T * PACK], BF16, name="x_bf%d" % g, align_bytes=64)
+            border = T - SCALAR_COLS
+            for round_on, c0, c1 in (
+                (round_on_scalar, border, T),
+                (round_on_vector, 0, X_COLS),
+                (round_on_vector, X_COLS, border),
+            ):
                 round_on(
-                    rounded[:, c0:c1, :].rearrange("p (c i) j -> p c j i", i=LINE),
-                    x_raw[g, half][:, :, c0:c1].rearrange("p j (c i) -> p c j i", i=LINE),
+                    rounded[:, c0 * PACK : c1 * PACK].rearrange("p (c i j) -> p c j i", i=LINE, j=PACK),
+                    x_raw[g][:, :, c0:c1].rearrange("p j (c i) -> p c j i", i=LINE),
                 )
-            cols = slice(half * X_COLS, (half + 1) * X_COLS)
-            nc.vector.quantize_mx(
-                out=x_words[g][:, cols].bitcast(FP8X4),
-                scales=x_scales[SCALE_ROWS * g : P, cols],
-                in_=rounded[:].rearrange("p c j -> p (c j)"),
-            )
+            for half in range(2):
+                cols = slice(half * X_COLS, (half + 1) * X_COLS)
+                nc.vector.quantize_mx(
+                    out=x_words[g][:, cols].bitcast(FP8X4),
+                    scales=x_scales[SCALE_ROWS * g : P, cols],
+                    in_=rounded[:, cols.start * PACK : cols.stop * PACK],
+                )
 
         def pick(picked, table):
             nc.vector.tensor_copy(picked[:], table[:].indirect(offsets[:]))
 
-        quantise_tokens(0, 0, SCALAR_COLS)
-        quantise_tokens(0, 1, SCALAR_COLS)
+        quantise_tokens(0)
         pick(picked_words[0], x_words[0])
-        quantise_tokens(1, 0, SCALAR_COLS)
-        quantise_tokens(1, 1, SCALAR_COLS_LAST)
+        quantise_tokens(1)
         pick(picked_scales, x_scales)
         pick(picked_words[1], x_words[1])
 

@@ -67,9 +67,9 @@ def tile_picked_route2_glusilu_e_kernel(tc, xT, gate, w1, w3, w2_words, w2_scale
         nc.sync.dma_start(offsets[:], offs)
         x_raw[1] = load(xT, 1, 0, T, "x_raw1")
         w_raw = {}
-        for mat, g in ((W1, 0), (W1, 1), (W3, 0)):
-            w_raw[mat, g] = [load((w1, w3)[mat], g, 0, H, "w_raw%d%d" % (mat, g))]
-        w_raw[W3, 1] = [load(w3, 1, half * H // 2, H // 2, "w_last%d" % half) for half in range(2)]
+        for mat in (W1, W3):
+            for g in range(PASSES):
+                w_raw[mat, g] = load((w1, w3)[mat], g, 0, H, "w_raw%d%d" % (mat, g))
         w2_codes = keep.tile([P, 2 * N], U8, name="w2_codes", align_bytes=64)
         nc.sync.dma_start(w2_codes[:].bitcast(I32), w2_words[0].bitcast(I32))
         for q in range(P // 32):
@@ -117,37 +117,28 @@ def tile_picked_route2_glusilu_e_kernel(tc, xT, gate, w1, w3, w2_words, w2_scale
 
         w_words, w_scales = {}, {}
 
-        def quantise_weights(mat, g, round_low, round_high):
+        def quantise_weights(mat, g, vector_cols, calls):
             words = keep.tile([P, H], U32, name="w_words%d%d" % (mat, g), align_bytes=64)
             scales = keep.tile([P, H], U8, name="w_scales%d%d" % (mat, g), align_bytes=64)
             w_words[mat, g], w_scales[mat, g] = words, scales
-            pieces = w_raw[mat, g]
-            m_cols = P // len(pieces)
-            for piece, raw in enumerate(pieces):
-                rounded = {}
-                for pair, round_on in enumerate((round_low, round_high)):
-                    rounded[pair] = keep.tile(
-                        [P, 2, m_cols, PACK], BF16, name="w_bf%d%d%d%d" % (mat, g, piece, pair), align_bytes=64
-                    )
-                    round_on(
-                        rounded[pair][:].rearrange("p u m j -> p m j u"),
-                        raw[:].rearrange("p j (m t) -> p m j t", t=PACK)[:, :, :, 2 * pair : 2 * pair + 2],
-                    )
-                for pair in range(2):
-                    if m_cols == P:
-                        runs = [(2 * pair * P, 2 * P, rounded[pair][:].rearrange("p u m j -> p (u m j)"))]
-                    else:
-                        runs = [
-                            (
-                                (2 * pair + u) * P + piece * m_cols,
-                                m_cols,
-                                rounded[pair][:, u, :, :].rearrange("p m j -> p (m j)"),
-                            )
-                            for u in range(2)
-                        ]
-                    for first, width, values in runs:
-                        cols = slice(first, first + width)
-                        nc.vector.quantize_mx(out=words[:, cols].bitcast(FP8X4), scales=scales[:, cols], in_=values)
+            dealt = w_raw[mat, g][:].rearrange("p j (m t) -> p m j t", t=PACK)
+            rounded = keep.tile([P, PACK, P, PACK], BF16, name="w_bf%d%d" % (mat, g), align_bytes=64)
+            for pair in range(2):
+                border = min(max(vector_cols - pair * P, 0), P)
+                for round_on, m0, m1 in ((round_on_vector, 0, border), (round_on_scalar, border, P)):
+                    if m1 > m0:
+                        round_on(
+                            rounded[:, 2 * pair : 2 * pair + 2, m0:m1, :].rearrange("p u m j -> p m j u"),
+                            dealt[:, m0:m1, :, 2 * pair : 2 * pair + 2],
+                        )
+            for call in range(calls):
+                tiles = slice(call * PACK // calls, (call + 1) * PACK // calls)
+                cols = slice(tiles.start * P, tiles.stop * P)
+                nc.vector.quantize_mx(
+                    out=words[:, cols].bitcast(FP8X4),
+                    scales=scales[:, cols],
+                    in_=rounded[:, tiles, :, :].rearrange("p t m j -> p (t m j)"),
+                )
 
         def first_layer_pass(acc, mat, g, t, tokens):
             cols = slice(t * P, (t + 1) * P)
@@ -161,7 +152,7 @@ def tile_picked_route2_glusilu_e_kernel(tc, xT, gate, w1, w3, w2_words, w2_scale
                 stop=(g == PASSES - 1),
             )
 
-        quantise_weights(W1, 0, round_on_scalar, round_on_scalar)
+        quantise_weights(W1, 0, 0, 1)
         w1_banks = {}
         for half in range(2):
             for pair in range(2):
@@ -175,16 +166,16 @@ def tile_picked_route2_glusilu_e_kernel(tc, xT, gate, w1, w3, w2_words, w2_scale
         for pair in range(2):
             for half in range(2):
                 w1_pass(half, pair, 0, 0)
-        quantise_weights(W1, 1, round_on_vector, round_on_scalar)
+        quantise_weights(W1, 1, 48, 1)
         for half in range(2):
             for pair in range(2):
                 for u, g in ((0, 1), (1, 0), (1, 1)):
                     w1_pass(half, pair, u, g)
 
-        quantise_weights(W3, 0, round_on_vector, round_on_scalar)
-        quantise_weights(W3, 1, round_on_vector, round_on_scalar)
+        quantise_weights(W3, 0, 112, 1)
+        quantise_weights(W3, 1, 144, 2)
 
-        silu_w1 = keep.tile([P, CHUNKS, 2, CHUNK, 2], F32, name="silu_w1", tag="w_last1")
+        silu_w1 = keep.tile([P, CHUNKS, 2, CHUNK, 2], F32, name="silu_w1", tag="w_raw11")
         for c in range(CHUNKS):
             for pair in range(2):
                 sums = w1_banks[c // 2, pair][:, :, (c % 2) * CHUNK : (c % 2 + 1) * CHUNK]
@@ -203,63 +194,60 @@ def tile_picked_route2_glusilu_e_kernel(tc, xT, gate, w1, w3, w2_words, w2_scale
                 for g in range(PASSES):
                     w3_pass(c, t, g)
 
-        hidden, h_codes = {}, {}
+        hidden = keep.tile([P, S * PACK], BF16, name="hidden", align_bytes=64)
+        h_words = keep.tile([P, S], U32, name="h_words", align_bytes=64)
+        h_scales = keep.tile([P, S], U8, name="h_scales", align_bytes=64)
         results = keep.tile([P, S], F32, name="results")
 
         def gated_product(c):
-            hidden[c] = keep.tile([P, CHUNK, PACK], BF16, name="hidden%d" % c, align_bytes=64)
             nc.vector.tensor_tensor(
-                hidden[c][:].rearrange("p c (r u) -> p c r u", u=2),
+                hidden[:, c * CHUNK * PACK : (c + 1) * CHUNK * PACK].rearrange("p (c r u) -> p c r u", r=2, u=2),
                 w3_banks[c][:].rearrange("p (r u) c -> p c r u", u=2),
                 silu_w1[:, c, :, :, :].rearrange("p r c u -> p c r u"),
                 MULT,
             )
 
-        def quantise_hidden(c):
-            words = keep.tile([P, CHUNK], U32, name="h_words%d" % c, align_bytes=64)
-            scales = keep.tile([P, CHUNK], U8, name="h_scales%d" % c, align_bytes=64)
+        def quantise_hidden(c0, c1):
+            cols = slice(c0 * CHUNK, c1 * CHUNK)
             nc.vector.quantize_mx(
-                out=words[:].bitcast(FP8X4), scales=scales[:], in_=hidden[c][:].rearrange("p c t -> p (c t)")
+                out=h_words[:, cols].bitcast(FP8X4),
+                scales=h_scales[:, cols],
+                in_=hidden[:, cols.start * PACK : cols.stop * PACK],
             )
-            h_codes[c] = words, scales
 
-        y_tags = ("w3_bank2", "w3_bank3", "w1_bank0", "w1_bank1")
-
-        def second_layer(c):
-            words, scales = h_codes[c]
-            y_bank = psum.tile([P, CHUNK], F32, name="y_bank%d" % c, tag=y_tags[c])
+        def second_layer(half):
+            cols = slice(half * S // 2, (half + 1) * S // 2)
+            y_bank = psum.tile([P, S // 2], F32, name="y_bank%d" % half, tag="w1_bank%d" % half)
             nc.tensor.matmul_mx(
                 out=y_bank[:],
                 lhsT=w2_codes[:].bitcast(FP4X4),
                 lhsT_scale=w2_plane[:],
-                rhs=words[:].bitcast(FP8X4),
-                rhs_scale=scales[:],
+                rhs=h_words[:, cols].bitcast(FP8X4),
+                rhs_scale=h_scales[:, cols],
                 start=True,
                 stop=True,
             )
-            nc.scalar.activation(results[:, c * CHUNK : (c + 1) * CHUNK], y_bank[:], ACT.Copy)
+            nc.scalar.activation(results[:, cols], y_bank[:], ACT.Copy)
 
-        def put(c0, c1):
+        def put(half):
+            cols = slice(half * S // 2, (half + 1) * S // 2)
             nc.vector.tensor_tensor(
-                window[:].indirect(places[:, c0 * LIST_COLS : c1 * LIST_COLS]),
-                results[:, c0 * CHUNK : c1 * CHUNK],
-                gates[:, c0 * CHUNK : c1 * CHUNK],
+                window[:].indirect(places[:, cols.start // LIST_ROWS : cols.stop // LIST_ROWS]),
+                results[:, cols],
+                gates[:, cols],
                 MULT,
             )
 
         gated_product(0)
         gated_product(1)
-        quantise_hidden(0)
         gated_product(2)
+        quantise_hidden(0, 2)
         second_layer(0)
-        quantise_hidden(1)
         gated_product(3)
+        quantise_hidden(2, 3)
+        quantise_hidden(3, 4)
         second_layer(1)
-        quantise_hidden(2)
-        second_layer(2)
-        put(0, 1)
-        quantise_hidden(3)
-        second_layer(3)
-        put(1, CHUNKS)
+        put(0)
+        put(1)
 
         nc.sync.dma_start(out, window[:])

@@ -109,36 +109,43 @@ def tile_picked_route2_glusilu_e_kernel(tc, xT, gate, w1, w3, w2_words, w2_scale
         def pick(picked, table):
             nc.vector.tensor_copy(picked[:], table[:].indirect(offsets[:]))
 
-        quantise_tokens(0)
-        pick(picked_words[0], x_words[0])
-        quantise_tokens(1)
-        pick(picked_scales, x_scales)
-        pick(picked_words[1], x_words[1])
-
         w_words, w_scales = {}, {}
 
-        def quantise_weights(mat, g, vector_cols, calls):
-            words = keep.tile([P, H], U32, name="w_words%d%d" % (mat, g), align_bytes=64)
-            scales = keep.tile([P, H], U8, name="w_scales%d%d" % (mat, g), align_bytes=64)
-            w_words[mat, g], w_scales[mat, g] = words, scales
+        w_rounded = {}
+
+        def round_weights(mat, g, vector_cols):
             dealt = w_raw[mat, g][:].rearrange("p j (m t) -> p m j t", t=PACK)
             rounded = keep.tile([P, PACK, P, PACK], BF16, name="w_bf%d%d" % (mat, g), align_bytes=64)
+            w_rounded[mat, g] = rounded
             for pair in range(2):
-                border = min(max(vector_cols - pair * P, 0), P)
-                for round_on, m0, m1 in ((round_on_vector, 0, border), (round_on_scalar, border, P)):
+                lo = min(max(vector_cols.start - pair * P, 0), P)
+                hi = min(max(vector_cols.stop - pair * P, 0), P)
+                for round_on, m0, m1 in ((round_on_scalar, 0, lo), (round_on_vector, lo, hi), (round_on_scalar, hi, P)):
                     if m1 > m0:
                         round_on(
                             rounded[:, 2 * pair : 2 * pair + 2, m0:m1, :].rearrange("p u m j -> p m j u"),
                             dealt[:, m0:m1, :, 2 * pair : 2 * pair + 2],
                         )
-            for call in range(calls):
-                tiles = slice(call * PACK // calls, (call + 1) * PACK // calls)
+
+        def quantise_weights(mat, g, borders):
+            words = keep.tile([P, H], U32, name="w_words%d%d" % (mat, g), align_bytes=64)
+            scales = keep.tile([P, H], U8, name="w_scales%d%d" % (mat, g), align_bytes=64)
+            w_words[mat, g], w_scales[mat, g] = words, scales
+            for first, last in zip(borders, borders[1:]):
+                tiles = slice(first, last)
                 cols = slice(tiles.start * P, tiles.stop * P)
                 nc.vector.quantize_mx(
                     out=words[:, cols].bitcast(FP8X4),
                     scales=scales[:, cols],
-                    in_=rounded[:, tiles, :, :].rearrange("p t m j -> p (t m j)"),
+                    in_=w_rounded[mat, g][:, tiles, :, :].rearrange("p t m j -> p (t m j)"),
                 )
+
+        quantise_tokens(0)
+        pick(picked_words[0], x_words[0])
+        quantise_tokens(1)
+        round_weights(W1, 0, slice(208, 256))
+        pick(picked_scales, x_scales)
+        pick(picked_words[1], x_words[1])
 
         def first_layer_pass(acc, mat, g, t, tokens):
             cols = slice(t * P, (t + 1) * P)
@@ -152,7 +159,7 @@ def tile_picked_route2_glusilu_e_kernel(tc, xT, gate, w1, w3, w2_words, w2_scale
                 stop=(g == PASSES - 1),
             )
 
-        quantise_weights(W1, 0, 0, 1)
+        quantise_weights(W1, 0, (0, 4))
         w1_banks = {}
         for half in range(2):
             for pair in range(2):
@@ -166,14 +173,17 @@ def tile_picked_route2_glusilu_e_kernel(tc, xT, gate, w1, w3, w2_words, w2_scale
         for pair in range(2):
             for half in range(2):
                 w1_pass(half, pair, 0, 0)
-        quantise_weights(W1, 1, 48, 1)
+        round_weights(W1, 1, slice(160, 256))
+        quantise_weights(W1, 1, (0, 2, 4))
         for half in range(2):
             for pair in range(2):
                 for u, g in ((0, 1), (1, 0), (1, 1)):
                     w1_pass(half, pair, u, g)
 
-        quantise_weights(W3, 0, 112, 1)
-        quantise_weights(W3, 1, 144, 2)
+        round_weights(W3, 0, slice(128, 256))
+        quantise_weights(W3, 0, (0, 2, 4))
+        round_weights(W3, 1, slice(0, 160))
+        quantise_weights(W3, 1, (0, 2, 3, 4))
 
         silu_w1 = keep.tile([P, CHUNKS, 2, CHUNK, 2], F32, name="silu_w1", tag="w_raw11")
         for c in range(CHUNKS):

@@ -26,7 +26,7 @@ LINE = 4
 W1, W3 = 0, 1
 
 X_COLS = T // 2
-SCALAR_COLS = 448
+SCALAR_COLS = 480
 
 CHUNK = 128
 CHUNKS = S // CHUNK
@@ -80,7 +80,9 @@ def tile_picked_route2_glusilu_e_kernel(tc, xT, gate, w1, w3, w2_words, w2_scale
         places = keep.tile([P, S // LIST_ROWS], U16, name="places")
         nc.sync.dma_start(places[:], dst)
         gates = keep.tile([P, S], F32, name="gates")
-        nc.sync.dma_start(gates[:], gate)
+        for half in range(2):
+            cols = slice(half * S // 2, (half + 1) * S // 2)
+            nc.sync.dma_start(gates[:, cols], gate[:, cols])
 
         x_words = [keep.tile([P, T], U32, name="x_words%d" % g, align_bytes=64) for g in range(PASSES)]
         picked_words = [keep.tile([P, S], U32, name="picked_words%d" % g, align_bytes=64) for g in range(PASSES)]
@@ -90,7 +92,8 @@ def tile_picked_route2_glusilu_e_kernel(tc, xT, gate, w1, w3, w2_words, w2_scale
             rounded = keep.tile([P, T * PACK], BF16, name="x_bf%d" % g, align_bytes=64)
             border = T - SCALAR_COLS
             for round_on, c0, c1 in (
-                (round_on_scalar, border, T),
+                (round_on_scalar, border, 3 * T // 4),
+                (round_on_scalar, 3 * T // 4, T),
                 (round_on_vector, 0, X_COLS),
                 (round_on_vector, X_COLS, border),
             ):
@@ -98,8 +101,8 @@ def tile_picked_route2_glusilu_e_kernel(tc, xT, gate, w1, w3, w2_words, w2_scale
                     rounded[:, c0 * PACK : c1 * PACK].rearrange("p (c i j) -> p c j i", i=LINE, j=PACK),
                     x_raw[g][:, :, c0:c1].rearrange("p j (c i) -> p c j i", i=LINE),
                 )
-            for half in range(2):
-                cols = slice(half * X_COLS, (half + 1) * X_COLS)
+            for c0, c1 in ((0, X_COLS), (X_COLS, 3 * T // 4), (3 * T // 4, T)):
+                cols = slice(c0, c1)
                 nc.vector.quantize_mx(
                     out=x_words[g][:, cols].bitcast(FP8X4),
                     scales=x_scales[SCALE_ROWS * g : P, cols],
@@ -182,7 +185,7 @@ def tile_picked_route2_glusilu_e_kernel(tc, xT, gate, w1, w3, w2_words, w2_scale
 
         round_weights(W3, 0, slice(128, 256))
         quantise_weights(W3, 0, (0, 2, 4))
-        round_weights(W3, 1, slice(0, 160))
+        round_weights(W3, 1, slice(0, 168))
         quantise_weights(W3, 1, (0, 2, 3, 4))
 
         silu_w1 = keep.tile([P, CHUNKS, 2, CHUNK, 2], F32, name="silu_w1", tag="w_raw11")

@@ -25,12 +25,20 @@ SCALE_ROWS = 4
 LINE = 4
 W1, W3 = 0, 1
 
-X_COLS = T // 2
-SCALAR_COLS = 480
+QUADRANT = 32
+PAIRS = 2
+
+VECTOR_TOKENS = 544
+VECTOR_COLS = {
+    (W1, 0): slice(208, 256),
+    (W1, 1): slice(160, 256),
+    (W3, 0): slice(128, 256),
+    (W3, 1): slice(0, 168),
+}
 
 CHUNK = 128
 CHUNKS = S // CHUNK
-LIST_COLS = CHUNK // LIST_ROWS
+SCATTERS = ((0, 1), (1, CHUNKS))
 
 
 def tile_picked_route2_glusilu_e_kernel(tc, xT, gate, w1, w3, w2_words, w2_scales, offs, dst, out):
@@ -40,11 +48,14 @@ def tile_picked_route2_glusilu_e_kernel(tc, xT, gate, w1, w3, w2_words, w2_scale
         keep = ctx.enter_context(tc.tile_pool(name="keep", bufs=1))
         psum = ctx.enter_context(tc.psum_pool(name="psum", bufs=1))
 
-        def load(src, g, first, width, name):
-            raw = keep.tile([P, PACK, width], F32, name=name, tag=name)
+        def load_pass(src, g, name):
+            raw = keep.tile([P, PACK, src.shape[1]], F32, name=name, tag=name)
             rows = src[g * K_PASS : (g + 1) * K_PASS, :].rearrange("(p j) c -> p j c", j=PACK)
-            nc.sync.dma_start(out=raw[:], in_=rows[:, :, first : first + width])
+            nc.sync.dma_start(out=raw[:], in_=rows)
             return raw
+
+        def chunk_cols(c0, c1, per_token=1):
+            return slice(c0 * CHUNK * per_token, c1 * CHUNK * per_token)
 
         def round_on_scalar(rounded, raw):
             nc.scalar.activation(rounded, raw, ACT.Copy)
@@ -62,27 +73,26 @@ def tile_picked_route2_glusilu_e_kernel(tc, xT, gate, w1, w3, w2_words, w2_scale
         warm = keep.tile([P, 8], F32, name="warm")
         nc.scalar.activation(warm[:], window[:, 0:8], ACT.Silu)
 
-        x_raw = {0: load(xT, 0, 0, T, "x_raw0")}
+        x_raw = {0: load_pass(xT, 0, "x_raw0")}
         offsets = keep.tile([P, S // LIST_ROWS], U16, name="offsets")
         nc.sync.dma_start(offsets[:], offs)
-        x_raw[1] = load(xT, 1, 0, T, "x_raw1")
+        x_raw[1] = load_pass(xT, 1, "x_raw1")
         w_raw = {}
         for mat in (W1, W3):
             for g in range(PASSES):
-                w_raw[mat, g] = load((w1, w3)[mat], g, 0, H, "w_raw%d%d" % (mat, g))
+                w_raw[mat, g] = load_pass((w1, w3)[mat], g, "w_raw%d%d" % (mat, g))
         w2_codes = keep.tile([P, 2 * N], U8, name="w2_codes", align_bytes=64)
         nc.sync.dma_start(w2_codes[:].bitcast(I32), w2_words[0].bitcast(I32))
-        for q in range(P // 32):
+        for q in range(P // QUADRANT):
             nc.sync.dma_start(
-                w2_plane[32 * q : 32 * q + SCALE_ROWS, :].bitcast(I32),
+                w2_plane[QUADRANT * q : QUADRANT * q + SCALE_ROWS, :].bitcast(I32),
                 w2_scales[0, SCALE_ROWS * q : SCALE_ROWS * (q + 1), :].bitcast(I32),
             )
         places = keep.tile([P, S // LIST_ROWS], U16, name="places")
         nc.sync.dma_start(places[:], dst)
         gates = keep.tile([P, S], F32, name="gates")
-        for half in range(2):
-            cols = slice(half * S // 2, (half + 1) * S // 2)
-            nc.sync.dma_start(gates[:, cols], gate[:, cols])
+        for c0, c1 in SCATTERS:
+            nc.sync.dma_start(gates[:, chunk_cols(c0, c1)], gate[:, chunk_cols(c0, c1)])
 
         x_words = [keep.tile([P, T], U32, name="x_words%d" % g, align_bytes=64) for g in range(PASSES)]
         picked_words = [keep.tile([P, S], U32, name="picked_words%d" % g, align_bytes=64) for g in range(PASSES)]
@@ -90,37 +100,35 @@ def tile_picked_route2_glusilu_e_kernel(tc, xT, gate, w1, w3, w2_words, w2_scale
 
         def quantise_tokens(g):
             rounded = keep.tile([P, T * PACK], BF16, name="x_bf%d" % g, align_bytes=64)
-            border = T - SCALAR_COLS
+            middle, last_quarter = T // 2, 3 * T // 4
             for round_on, c0, c1 in (
-                (round_on_scalar, border, 3 * T // 4),
-                (round_on_scalar, 3 * T // 4, T),
-                (round_on_vector, 0, X_COLS),
-                (round_on_vector, X_COLS, border),
+                (round_on_scalar, VECTOR_TOKENS, last_quarter),
+                (round_on_scalar, last_quarter, T),
+                (round_on_vector, 0, middle),
+                (round_on_vector, middle, VECTOR_TOKENS),
             ):
                 round_on(
                     rounded[:, c0 * PACK : c1 * PACK].rearrange("p (c i j) -> p c j i", i=LINE, j=PACK),
                     x_raw[g][:, :, c0:c1].rearrange("p j (c i) -> p c j i", i=LINE),
                 )
-            for c0, c1 in ((0, X_COLS), (X_COLS, 3 * T // 4), (3 * T // 4, T)):
-                cols = slice(c0, c1)
+            for c0, c1 in ((0, middle), (middle, last_quarter), (last_quarter, T)):
                 nc.vector.quantize_mx(
-                    out=x_words[g][:, cols].bitcast(FP8X4),
-                    scales=x_scales[SCALE_ROWS * g : P, cols],
-                    in_=rounded[:, cols.start * PACK : cols.stop * PACK],
+                    out=x_words[g][:, c0:c1].bitcast(FP8X4),
+                    scales=x_scales[SCALE_ROWS * g : P, c0:c1],
+                    in_=rounded[:, c0 * PACK : c1 * PACK],
                 )
 
         def pick(picked, table):
             nc.vector.tensor_copy(picked[:], table[:].indirect(offsets[:]))
 
-        w_words, w_scales = {}, {}
+        w_rounded, w_words, w_scales = {}, {}, {}
 
-        w_rounded = {}
-
-        def round_weights(mat, g, vector_cols):
+        def round_weights(mat, g):
+            vector_cols = VECTOR_COLS[mat, g]
             dealt = w_raw[mat, g][:].rearrange("p j (m t) -> p m j t", t=PACK)
             rounded = keep.tile([P, PACK, P, PACK], BF16, name="w_bf%d%d" % (mat, g), align_bytes=64)
             w_rounded[mat, g] = rounded
-            for pair in range(2):
+            for pair in range(PAIRS):
                 lo = min(max(vector_cols.start - pair * P, 0), P)
                 hi = min(max(vector_cols.stop - pair * P, 0), P)
                 for round_on, m0, m1 in ((round_on_scalar, 0, lo), (round_on_vector, lo, hi), (round_on_scalar, hi, P)):
@@ -135,18 +143,17 @@ def tile_picked_route2_glusilu_e_kernel(tc, xT, gate, w1, w3, w2_words, w2_scale
             scales = keep.tile([P, H], U8, name="w_scales%d%d" % (mat, g), align_bytes=64)
             w_words[mat, g], w_scales[mat, g] = words, scales
             for first, last in zip(borders, borders[1:]):
-                tiles = slice(first, last)
-                cols = slice(tiles.start * P, tiles.stop * P)
+                cols = slice(first * P, last * P)
                 nc.vector.quantize_mx(
                     out=words[:, cols].bitcast(FP8X4),
                     scales=scales[:, cols],
-                    in_=w_rounded[mat, g][:, tiles, :, :].rearrange("p t m j -> p (t m j)"),
+                    in_=w_rounded[mat, g][:, first:last, :, :].rearrange("p t m j -> p (t m j)"),
                 )
 
         quantise_tokens(0)
         pick(picked_words[0], x_words[0])
         quantise_tokens(1)
-        round_weights(W1, 0, slice(208, 256))
+        round_weights(W1, 0)
         pick(picked_scales, x_scales)
         pick(picked_words[1], x_words[1])
 
@@ -162,42 +169,42 @@ def tile_picked_route2_glusilu_e_kernel(tc, xT, gate, w1, w3, w2_words, w2_scale
                 stop=(g == PASSES - 1),
             )
 
-        quantise_weights(W1, 0, (0, 4))
+        quantise_weights(W1, 0, (0, PACK))
         w1_banks = {}
         for half in range(2):
-            for pair in range(2):
-                name = "w1_bank%d" % (2 * half + pair)
+            for pair in range(PAIRS):
+                name = "w1_bank%d" % (PAIRS * half + pair)
                 w1_banks[half, pair] = psum.tile([P, 2, S // 2], F32, name=name, tag=name)
 
         def w1_pass(half, pair, u, g):
             tokens = slice(half * S // 2, (half + 1) * S // 2)
             first_layer_pass(w1_banks[half, pair][:, u, :], W1, g, 2 * pair + u, tokens)
 
-        for pair in range(2):
+        for pair in range(PAIRS):
             for half in range(2):
                 w1_pass(half, pair, 0, 0)
-        round_weights(W1, 1, slice(160, 256))
-        quantise_weights(W1, 1, (0, 2, 4))
+        round_weights(W1, 1)
+        quantise_weights(W1, 1, (0, 2, PACK))
         for half in range(2):
-            for pair in range(2):
+            for pair in range(PAIRS):
                 for u, g in ((0, 1), (1, 0), (1, 1)):
                     w1_pass(half, pair, u, g)
 
-        round_weights(W3, 0, slice(128, 256))
-        quantise_weights(W3, 0, (0, 2, 4))
-        round_weights(W3, 1, slice(0, 168))
-        quantise_weights(W3, 1, (0, 2, 3, 4))
+        round_weights(W3, 0)
+        quantise_weights(W3, 0, (0, 2, PACK))
+        round_weights(W3, 1)
+        quantise_weights(W3, 1, (0, 2, 3, PACK))
 
-        silu_w1 = keep.tile([P, CHUNKS, 2, CHUNK, 2], F32, name="silu_w1", tag="w_raw11")
+        silu_w1 = keep.tile([P, CHUNKS, PAIRS, CHUNK, 2], F32, name="silu_w1", tag="w_raw%d%d" % (W3, PASSES - 1))
         for c in range(CHUNKS):
-            for pair in range(2):
-                sums = w1_banks[c // 2, pair][:, :, (c % 2) * CHUNK : (c % 2 + 1) * CHUNK]
+            for pair in range(PAIRS):
+                sums = w1_banks[c // 2, pair][:, :, chunk_cols(c % 2, c % 2 + 1)]
                 nc.scalar.activation(silu_w1[:, c, pair, :, :], sums.rearrange("p u c -> p c u"), ACT.Silu)
 
         w3_banks = [psum.tile([P, PACK, CHUNK], F32, name="w3_bank%d" % c, tag="w3_bank%d" % c) for c in range(CHUNKS)]
 
         def w3_pass(c, t, g):
-            first_layer_pass(w3_banks[c][:, t, :], W3, g, t, slice(c * CHUNK, (c + 1) * CHUNK))
+            first_layer_pass(w3_banks[c][:, t, :], W3, g, t, chunk_cols(c, c + 1))
 
         for c in range(CHUNKS):
             w3_pass(c, 0, 0)
@@ -214,23 +221,23 @@ def tile_picked_route2_glusilu_e_kernel(tc, xT, gate, w1, w3, w2_words, w2_scale
 
         def gated_product(c):
             nc.vector.tensor_tensor(
-                hidden[:, c * CHUNK * PACK : (c + 1) * CHUNK * PACK].rearrange("p (c r u) -> p c r u", r=2, u=2),
+                hidden[:, chunk_cols(c, c + 1, PACK)].rearrange("p (c r u) -> p c r u", r=2, u=2),
                 w3_banks[c][:].rearrange("p (r u) c -> p c r u", u=2),
                 silu_w1[:, c, :, :, :].rearrange("p r c u -> p c r u"),
                 MULT,
             )
 
         def quantise_hidden(c0, c1):
-            cols = slice(c0 * CHUNK, c1 * CHUNK)
+            cols = chunk_cols(c0, c1)
             nc.vector.quantize_mx(
                 out=h_words[:, cols].bitcast(FP8X4),
                 scales=h_scales[:, cols],
-                in_=hidden[:, cols.start * PACK : cols.stop * PACK],
+                in_=hidden[:, chunk_cols(c0, c1, PACK)],
             )
 
-        def second_layer(half):
-            cols = slice(half * S // 2, (half + 1) * S // 2)
-            y_bank = psum.tile([P, S // 2], F32, name="y_bank%d" % half, tag="w1_bank%d" % half)
+        def second_layer(c0, c1, bank_tag):
+            cols = chunk_cols(c0, c1)
+            y_bank = psum.tile([P, (c1 - c0) * CHUNK], F32, name="y_bank%d" % c0, tag=bank_tag)
             nc.tensor.matmul_mx(
                 out=y_bank[:],
                 lhsT=w2_codes[:].bitcast(FP4X4),
@@ -242,8 +249,8 @@ def tile_picked_route2_glusilu_e_kernel(tc, xT, gate, w1, w3, w2_words, w2_scale
             )
             nc.scalar.activation(results[:, cols], y_bank[:], ACT.Copy)
 
-        def put(half):
-            cols = slice(half * S // 2, (half + 1) * S // 2)
+        def put(c0, c1):
+            cols = chunk_cols(c0, c1)
             nc.vector.tensor_tensor(
                 window[:].indirect(places[:, cols.start // LIST_ROWS : cols.stop // LIST_ROWS]),
                 results[:, cols],
@@ -253,14 +260,15 @@ def tile_picked_route2_glusilu_e_kernel(tc, xT, gate, w1, w3, w2_words, w2_scale
 
         gated_product(0)
         gated_product(1)
+        quantise_hidden(0, 1)
         gated_product(2)
-        quantise_hidden(0, 2)
-        second_layer(0)
+        second_layer(0, 1, "w3_bank2")
         gated_product(3)
-        quantise_hidden(2, 3)
+        quantise_hidden(1, 3)
+        second_layer(1, 3, "w1_bank0")
         quantise_hidden(3, 4)
-        second_layer(1)
-        put(0)
-        put(1)
+        second_layer(3, 4, "w1_bank1")
+        for c0, c1 in SCATTERS:
+            put(c0, c1)
 
         nc.sync.dma_start(out, window[:])

@@ -73,10 +73,9 @@ def tile_picked_route2_glusilu_e_kernel(tc, xT, gate, w1, w3, w2_words, w2_scale
         warm = keep.tile([P, 8], F32, name="warm")
         nc.scalar.activation(warm[:], window[:, 0:8], ACT.Silu)
 
-        x_raw = {0: load_pass(xT, 0, "x_raw0")}
         offsets = keep.tile([P, S // LIST_ROWS], U16, name="offsets")
         nc.sync.dma_start(offsets[:], offs)
-        x_raw[1] = load_pass(xT, 1, "x_raw1")
+        x_raw = {g: load_pass(xT, g, "x_raw%d" % g) for g in range(PASSES)}
         w_raw = {}
         for mat in (W1, W3):
             for g in range(PASSES):
@@ -157,7 +156,7 @@ def tile_picked_route2_glusilu_e_kernel(tc, xT, gate, w1, w3, w2_words, w2_scale
         pick(picked_scales, x_scales)
         pick(picked_words[1], x_words[1])
 
-        def first_layer_pass(acc, mat, g, t, tokens):
+        def first_layer_pass(acc, mat, g, t, tokens, start, stop):
             cols = slice(t * P, (t + 1) * P)
             nc.tensor.matmul_mx(
                 out=acc,
@@ -165,8 +164,8 @@ def tile_picked_route2_glusilu_e_kernel(tc, xT, gate, w1, w3, w2_words, w2_scale
                 lhsT_scale=w_scales[mat, g][:, cols],
                 rhs=picked_words[g][:, tokens].bitcast(FP8X4),
                 rhs_scale=picked_scales[SCALE_ROWS * g : P, tokens],
-                start=(g == 0),
-                stop=(g == PASSES - 1),
+                start=start,
+                stop=stop,
             )
 
         quantise_weights(W1, 0, (0, PACK))
@@ -178,17 +177,18 @@ def tile_picked_route2_glusilu_e_kernel(tc, xT, gate, w1, w3, w2_words, w2_scale
 
         def w1_pass(half, pair, u, g):
             tokens = slice(half * S // 2, (half + 1) * S // 2)
-            first_layer_pass(w1_banks[half, pair][:, u, :], W1, g, 2 * pair + u, tokens)
+            first_layer_pass(w1_banks[half, pair][:, u, :], W1, g, 2 * pair + u, tokens, (g, u) == (0, 0), (g, u) == (PASSES - 1, 1))
 
         for pair in range(PAIRS):
-            for half in range(2):
-                w1_pass(half, pair, 0, 0)
+            for u in range(2):
+                for half in range(2):
+                    w1_pass(half, pair, u, 0)
         round_weights(W1, 1)
         quantise_weights(W1, 1, (0, 2, PACK))
         for half in range(2):
             for pair in range(PAIRS):
-                for u, g in ((0, 1), (1, 0), (1, 1)):
-                    w1_pass(half, pair, u, g)
+                for u in range(2):
+                    w1_pass(half, pair, u, 1)
 
         round_weights(W3, 0)
         quantise_weights(W3, 0, (0, 2, PACK))
@@ -203,16 +203,17 @@ def tile_picked_route2_glusilu_e_kernel(tc, xT, gate, w1, w3, w2_words, w2_scale
 
         w3_banks = [psum.tile([P, PACK, CHUNK], F32, name="w3_bank%d" % c, tag="w3_bank%d" % c) for c in range(CHUNKS)]
 
-        def w3_pass(c, t, g):
-            first_layer_pass(w3_banks[c][:, t, :], W3, g, t, chunk_cols(c, c + 1))
+        def w3_pass(c, t, g, first=False, last=False):
+            first_layer_pass(w3_banks[c][:, t, :], W3, g, t, chunk_cols(c, c + 1), first, last)
 
+        forward = [(t, g) for g in range(PASSES) for t in range(PACK)]
+        orders = [forward, forward[:PACK] + forward[: PACK - 1 : -1], forward[::-1], forward[::-1]]
+        for c in range(2):
+            for t, g in orders[c][:PACK]:
+                w3_pass(c, t, g, first=(t, g) == orders[c][0])
         for c in range(CHUNKS):
-            w3_pass(c, 0, 0)
-        for c in range(CHUNKS):
-            w3_pass(c, 0, 1)
-            for t in range(1, PACK):
-                for g in range(PASSES):
-                    w3_pass(c, t, g)
+            for t, g in orders[c][PACK if c < 2 else 0 :]:
+                w3_pass(c, t, g, first=(t, g) == orders[c][0], last=(t, g) == orders[c][-1])
 
         hidden = keep.tile([P, S * PACK], BF16, name="hidden", align_bytes=64)
         h_words = keep.tile([P, S], U32, name="h_words", align_bytes=64)

@@ -87,11 +87,11 @@ def tile_picked_route2_glusilu_e_kernel(tc, xT, gate, w1, w3, w2_words, w2_scale
                 w2_plane[QUADRANT * q : QUADRANT * q + SCALE_ROWS, :].bitcast(I32),
                 w2_scales[0, SCALE_ROWS * q : SCALE_ROWS * (q + 1), :].bitcast(I32),
             )
+        gates = keep.tile([P, S], F32, name="gates")
+        nc.sync.dma_start(gates[:, 0:CHUNK], gate[:, 0:CHUNK])
         places = keep.tile([P, S // LIST_ROWS], U16, name="places")
         nc.sync.dma_start(places[:], dst)
-        gates = keep.tile([P, S], F32, name="gates")
-        for c0, c1 in SCATTERS:
-            nc.sync.dma_start(gates[:, chunk_cols(c0, c1)], gate[:, chunk_cols(c0, c1)])
+        nc.sync.dma_start(gates[:, CHUNK:S], gate[:, CHUNK:S])
 
         x_words = [keep.tile([P, T], U32, name="x_words%d" % g, align_bytes=64) for g in range(PASSES)]
         picked_words = [keep.tile([P, S], U32, name="picked_words%d" % g, align_bytes=64) for g in range(PASSES)]
@@ -220,11 +220,12 @@ def tile_picked_route2_glusilu_e_kernel(tc, xT, gate, w1, w3, w2_words, w2_scale
         h_scales = keep.tile([P, S], U8, name="h_scales", align_bytes=64)
         results = keep.tile([P, S], F32, name="results")
 
-        def gated_product(c):
+        def gated_product(c, half=None):
+            tokens = slice(0, CHUNK) if half is None else slice(half * CHUNK // 2, (half + 1) * CHUNK // 2)
             nc.vector.tensor_tensor(
-                hidden[:, chunk_cols(c, c + 1, PACK)].rearrange("p (c r u) -> p c r u", r=2, u=2),
-                w3_banks[c][:].rearrange("p (r u) c -> p c r u", u=2),
-                silu_w1[:, c, :, :, :].rearrange("p r c u -> p c r u"),
+                hidden[:, chunk_cols(c, c + 1, PACK)].rearrange("p (c r u) -> p c r u", r=2, u=2)[:, tokens],
+                w3_banks[c][:, :, tokens].rearrange("p (r u) c -> p c r u", u=2),
+                silu_w1[:, c, :, tokens, :].rearrange("p r c u -> p c r u"),
                 MULT,
             )
 
@@ -236,9 +237,9 @@ def tile_picked_route2_glusilu_e_kernel(tc, xT, gate, w1, w3, w2_words, w2_scale
                 in_=hidden[:, chunk_cols(c0, c1, PACK)],
             )
 
-        def second_layer(c0, c1, bank_tag):
-            cols = chunk_cols(c0, c1)
-            y_bank = psum.tile([P, (c1 - c0) * CHUNK], F32, name="y_bank%d" % c0, tag=bank_tag)
+        def second_layer(c):
+            cols = chunk_cols(c, c + 1)
+            y_bank = psum.tile([P, CHUNK], F32, name="y_bank%d" % c, tag="w1_bank%d" % c)
             nc.tensor.matmul_mx(
                 out=y_bank[:],
                 lhsT=w2_codes[:].bitcast(FP4X4),
@@ -248,28 +249,41 @@ def tile_picked_route2_glusilu_e_kernel(tc, xT, gate, w1, w3, w2_words, w2_scale
                 start=True,
                 stop=True,
             )
-            nc.scalar.activation(results[:, cols], y_bank[:], ACT.Copy)
+            return y_bank
 
-        def put(c0, c1):
+        def put(c, y_bank):
+            cols = chunk_cols(c, c + 1)
+            nc.vector.tensor_tensor(results[:, cols], y_bank[:], gates[:, cols], MULT)
+
+        def scatter(c0, c1):
             cols = chunk_cols(c0, c1)
-            nc.vector.tensor_tensor(
+            nc.scalar.activation(
                 window[:].indirect(places[:, cols.start // LIST_ROWS : cols.stop // LIST_ROWS]),
                 results[:, cols],
-                gates[:, cols],
-                MULT,
+                ACT.Copy,
             )
 
         gated_product(0)
-        gated_product(1)
+        gated_product(1, 0)
         quantise_hidden(0, 1)
-        gated_product(2)
-        second_layer(0, 1, "w3_bank2")
-        gated_product(3)
-        quantise_hidden(1, 3)
-        second_layer(1, 3, "w1_bank0")
+        y0 = second_layer(0)
+        gated_product(1, 1)
+        gated_product(2, 0)
+        put(0, y0)
+        scatter(0, 1)
+        quantise_hidden(1, 2)
+        y1 = second_layer(1)
+        gated_product(2, 1)
+        gated_product(3, 0)
+        put(1, y1)
+        scatter(1, 2)
+        quantise_hidden(2, 3)
+        y2 = second_layer(2)
+        gated_product(3, 1)
+        put(2, y2)
         quantise_hidden(3, 4)
-        second_layer(3, 4, "w1_bank1")
-        for c0, c1 in SCATTERS:
-            put(c0, c1)
+        y3 = second_layer(3)
+        put(3, y3)
+        scatter(2, 4)
 
         nc.sync.dma_start(out, window[:])

@@ -38,7 +38,7 @@ VECTOR_COLS = {
 
 CHUNK = 128
 CHUNKS = S // CHUNK
-SCATTERS = ((0, 1), (1, CHUNKS))
+SCATTER_BORDERS = [0, 1, 2, CHUNKS]
 
 
 def tile_picked_route2_glusilu_e_kernel(tc, xT, gate, w1, w3, w2_words, w2_scales, offs, dst, out):
@@ -80,6 +80,8 @@ def tile_picked_route2_glusilu_e_kernel(tc, xT, gate, w1, w3, w2_words, w2_scale
         for mat in (W1, W3):
             for g in range(PASSES):
                 w_raw[mat, g] = load_pass((w1, w3)[mat], g, "w_raw%d%d" % (mat, g))
+        gates = keep.tile([P, S], F32, name="gates")
+        nc.sync.dma_start(gates[:], gate)
         w2_codes = keep.tile([P, 2 * N], U8, name="w2_codes", align_bytes=64)
         nc.sync.dma_start(w2_codes[:].bitcast(I32), w2_words[0].bitcast(I32))
         for q in range(P // QUADRANT):
@@ -87,11 +89,8 @@ def tile_picked_route2_glusilu_e_kernel(tc, xT, gate, w1, w3, w2_words, w2_scale
                 w2_plane[QUADRANT * q : QUADRANT * q + SCALE_ROWS, :].bitcast(I32),
                 w2_scales[0, SCALE_ROWS * q : SCALE_ROWS * (q + 1), :].bitcast(I32),
             )
-        gates = keep.tile([P, S], F32, name="gates")
-        nc.sync.dma_start(gates[:, 0:CHUNK], gate[:, 0:CHUNK])
         places = keep.tile([P, S // LIST_ROWS], U16, name="places")
         nc.sync.dma_start(places[:], dst)
-        nc.sync.dma_start(gates[:, CHUNK:S], gate[:, CHUNK:S])
 
         x_words = [keep.tile([P, T], U32, name="x_words%d" % g, align_bytes=64) for g in range(PASSES)]
         picked_words = [keep.tile([P, S], U32, name="picked_words%d" % g, align_bytes=64) for g in range(PASSES)]
@@ -215,37 +214,32 @@ def tile_picked_route2_glusilu_e_kernel(tc, xT, gate, w1, w3, w2_words, w2_scale
             for t, g in orders[c][PACK if c < 2 else 0 :]:
                 w3_pass(c, t, g, first=(t, g) == orders[c][0], last=(t, g) == orders[c][-1])
 
-        hidden = keep.tile([P, S * PACK], BF16, name="hidden", align_bytes=64)
-        h_words = keep.tile([P, S], U32, name="h_words", align_bytes=64)
-        h_scales = keep.tile([P, S], U8, name="h_scales", align_bytes=64)
         results = keep.tile([P, S], F32, name="results")
+        hidden = {}
 
-        def gated_product(c, half=None):
-            tokens = slice(0, CHUNK) if half is None else slice(half * CHUNK // 2, (half + 1) * CHUNK // 2)
+        def gated_product(c, first=0, last=CHUNK):
+            if first == 0:
+                hidden[c] = keep.tile([P, CHUNK, PACK], BF16, name="hidden%d" % c, tag="h_words0" if c == 3 else "hidden%d" % c, align_bytes=64)
             nc.vector.tensor_tensor(
-                hidden[:, chunk_cols(c, c + 1, PACK)].rearrange("p (c r u) -> p c r u", r=2, u=2)[:, tokens],
-                w3_banks[c][:, :, tokens].rearrange("p (r u) c -> p c r u", u=2),
-                silu_w1[:, c, :, tokens, :].rearrange("p r c u -> p c r u"),
+                hidden[c][:, first:last, :].rearrange("p c (r u) -> p c r u", u=2),
+                w3_banks[c][:, :, first:last].rearrange("p (r u) c -> p c r u", u=2),
+                silu_w1[:, c, :, first:last, :].rearrange("p r c u -> p c r u"),
                 MULT,
             )
 
-        def quantise_hidden(c0, c1):
-            cols = chunk_cols(c0, c1)
-            nc.vector.quantize_mx(
-                out=h_words[:, cols].bitcast(FP8X4),
-                scales=h_scales[:, cols],
-                in_=hidden[:, chunk_cols(c0, c1, PACK)],
-            )
-
         def second_layer(c):
-            cols = chunk_cols(c, c + 1)
+            words = keep.tile([P, CHUNK], U32, name="h_words%d" % c, tag="h_words%d" % c, align_bytes=64)
+            scales = keep.tile([P, CHUNK], U8, name="h_scales%d" % c, tag="h_scales%d" % (0 if c == 2 else c), align_bytes=64)
+            nc.vector.quantize_mx(
+                out=words[:].bitcast(FP8X4), scales=scales[:], in_=hidden[c][:].rearrange("p c t -> p (c t)")
+            )
             y_bank = psum.tile([P, CHUNK], F32, name="y_bank%d" % c, tag="w1_bank%d" % c)
             nc.tensor.matmul_mx(
                 out=y_bank[:],
                 lhsT=w2_codes[:].bitcast(FP4X4),
                 lhsT_scale=w2_plane[:],
-                rhs=h_words[:, cols].bitcast(FP8X4),
-                rhs_scale=h_scales[:, cols],
+                rhs=words[:].bitcast(FP8X4),
+                rhs_scale=scales[:],
                 start=True,
                 stop=True,
             )
@@ -254,6 +248,8 @@ def tile_picked_route2_glusilu_e_kernel(tc, xT, gate, w1, w3, w2_words, w2_scale
         def put(c, y_bank):
             cols = chunk_cols(c, c + 1)
             nc.vector.tensor_tensor(results[:, cols], y_bank[:], gates[:, cols], MULT)
+            if c + 1 in SCATTER_BORDERS:
+                scatter(SCATTER_BORDERS[SCATTER_BORDERS.index(c + 1) - 1], c + 1)
 
         def scatter(c0, c1):
             cols = chunk_cols(c0, c1)
@@ -264,26 +260,17 @@ def tile_picked_route2_glusilu_e_kernel(tc, xT, gate, w1, w3, w2_words, w2_scale
             )
 
         gated_product(0)
-        gated_product(1, 0)
-        quantise_hidden(0, 1)
-        y0 = second_layer(0)
-        gated_product(1, 1)
-        gated_product(2, 0)
-        put(0, y0)
-        scatter(0, 1)
-        quantise_hidden(1, 2)
-        y1 = second_layer(1)
-        gated_product(2, 1)
-        gated_product(3, 0)
-        put(1, y1)
-        scatter(1, 2)
-        quantise_hidden(2, 3)
-        y2 = second_layer(2)
-        gated_product(3, 1)
-        put(2, y2)
-        quantise_hidden(3, 4)
-        y3 = second_layer(3)
-        put(3, y3)
-        scatter(2, 4)
+        gated_product(1, 0, 64)
+        y_banks = {0: second_layer(0)}
+        gated_product(1, 64)
+        gated_product(2)
+        y_banks[1] = second_layer(1)
+        put(0, y_banks[0])
+        y_banks[2] = second_layer(2)
+        gated_product(3)
+        put(1, y_banks[1])
+        y_banks[3] = second_layer(3)
+        put(2, y_banks[2])
+        put(3, y_banks[3])
 
         nc.sync.dma_start(out, window[:])

@@ -68,7 +68,12 @@ def tile_picked_route2_glusilu_e_kernel(tc, xT, gate, w1, w3, w2_words, w2_scale
         x_scales = keep.tile([P, T], U8, name="x_scales", align_bytes=64)
         nc.vector.memset(x_scales[:].bitcast(I32), 0)
         w2_plane = keep.tile([P, N], U8, name="w2_plane", align_bytes=64)
-        nc.vector.memset(w2_plane[:].bitcast(I32), 0)
+        nc.gpsimd.memset(w2_plane[:].bitcast(I32), 0)
+        for q in range(P // QUADRANT):
+            nc.scalar.dma_start(
+                w2_plane[QUADRANT * q : QUADRANT * q + SCALE_ROWS, :].bitcast(I32),
+                w2_scales[0, SCALE_ROWS * q : SCALE_ROWS * (q + 1), :].bitcast(I32),
+            )
 
         warm = keep.tile([P, 8], F32, name="warm")
         nc.scalar.activation(warm[:], window[:, 0:8], ACT.Silu)
@@ -81,16 +86,12 @@ def tile_picked_route2_glusilu_e_kernel(tc, xT, gate, w1, w3, w2_words, w2_scale
             for g in range(PASSES):
                 w_raw[mat, g] = load_pass((w1, w3)[mat], g, "w_raw%d%d" % (mat, g))
         gates = keep.tile([P, S], F32, name="gates")
-        nc.sync.dma_start(gates[:], gate)
+        nc.sync.dma_start(gates[:, 0 : S // 2], gate[:, 0 : S // 2])
         w2_codes = keep.tile([P, 2 * N], U8, name="w2_codes", align_bytes=64)
         nc.sync.dma_start(w2_codes[:].bitcast(I32), w2_words[0].bitcast(I32))
-        for q in range(P // QUADRANT):
-            nc.sync.dma_start(
-                w2_plane[QUADRANT * q : QUADRANT * q + SCALE_ROWS, :].bitcast(I32),
-                w2_scales[0, SCALE_ROWS * q : SCALE_ROWS * (q + 1), :].bitcast(I32),
-            )
         places = keep.tile([P, S // LIST_ROWS], U16, name="places")
         nc.sync.dma_start(places[:], dst)
+        nc.sync.dma_start(gates[:, S // 2 : S], gate[:, S // 2 : S])
 
         x_words = [keep.tile([P, T], U32, name="x_words%d" % g, align_bytes=64) for g in range(PASSES)]
         picked_words = [keep.tile([P, S], U32, name="picked_words%d" % g, align_bytes=64) for g in range(PASSES)]

@@ -33,7 +33,7 @@ VECTOR_COLS = {
     (W1, 0): slice(208, 256),
     (W1, 1): slice(160, 256),
     (W3, 0): slice(128, 256),
-    (W3, 1): slice(0, 168),
+    (W3, 1): slice(0, 160),
 }
 
 CHUNK = 128
@@ -230,7 +230,7 @@ def tile_picked_route2_glusilu_e_kernel(tc, xT, gate, w1, w3, w2_words, w2_scale
 
         def second_layer(c):
             words = keep.tile([P, CHUNK], U32, name="h_words%d" % c, tag="h_words%d" % c, align_bytes=64)
-            scales = keep.tile([P, CHUNK], U8, name="h_scales%d" % c, tag="h_scales%d" % (0 if c == 2 else c), align_bytes=64)
+            scales = keep.tile([P, CHUNK], U8, name="h_scales%d" % c, tag="h_scales%d" % (c // 3), align_bytes=64)
             nc.vector.quantize_mx(
                 out=words[:].bitcast(FP8X4), scales=scales[:], in_=hidden[c][:].rearrange("p c t -> p (c t)")
             )
@@ -265,10 +265,10 @@ def tile_picked_route2_glusilu_e_kernel(tc, xT, gate, w1, w3, w2_words, w2_scale
         y_banks = {0: second_layer(0)}
         gated_product(1, 64)
         gated_product(2)
-        y_banks[1] = second_layer(1)
         put(0, y_banks[0])
-        y_banks[2] = second_layer(2)
+        y_banks[1] = second_layer(1)
         gated_product(3)
+        y_banks[2] = second_layer(2)
         put(1, y_banks[1])
         y_banks[3] = second_layer(3)
         put(2, y_banks[2])

@@ -78,9 +78,10 @@ def tile_picked_route2_glusilu_e_kernel(tc, xT, gate, w1, w3, w2_words, w2_scale
         warm = keep.tile([P, 8], F32, name="warm")
         nc.scalar.activation(warm[:], window[:, 0:8], ACT.Silu)
 
+        x_raw = {0: load_pass(xT, 0, "x_raw0")}
         offsets = keep.tile([P, S // LIST_ROWS], U16, name="offsets")
         nc.sync.dma_start(offsets[:], offs)
-        x_raw = {g: load_pass(xT, g, "x_raw%d" % g) for g in range(PASSES)}
+        x_raw[1] = load_pass(xT, 1, "x_raw1")
         w_raw = {}
         for mat in (W1, W3):
             for g in range(PASSES):
@@ -230,7 +231,7 @@ def tile_picked_route2_glusilu_e_kernel(tc, xT, gate, w1, w3, w2_words, w2_scale
 
         def second_layer(c):
             words = keep.tile([P, CHUNK], U32, name="h_words%d" % c, tag="h_words%d" % c, align_bytes=64)
-            scales = keep.tile([P, CHUNK], U8, name="h_scales%d" % c, tag="h_scales%d" % (c // 3), align_bytes=64)
+            scales = keep.tile([P, CHUNK], U8, name="h_scales%d" % c, tag="h_scales%d" % max(c - 1, 0), align_bytes=64)
             nc.vector.quantize_mx(
                 out=words[:].bitcast(FP8X4), scales=scales[:], in_=hidden[c][:].rearrange("p c t -> p (c t)")
             )

@@ -38,6 +38,7 @@ VECTOR_COLS = {
 
 CHUNK = 128
 CHUNKS = S // CHUNK
+HELD = 256
 SCATTER_BORDERS = [0, 1, 2, CHUNKS]
 
 
@@ -46,6 +47,7 @@ def tile_picked_route2_glusilu_e_kernel(tc, xT, gate, w1, w3, w2_words, w2_scale
 
     with ExitStack() as ctx:
         keep = ctx.enter_context(tc.tile_pool(name="keep", bufs=1))
+        held = ctx.enter_context(tc.tile_pool(name="held", bufs=1))
         psum = ctx.enter_context(tc.psum_pool(name="psum", bufs=1))
 
         def load_pass(src, g, name):
@@ -219,22 +221,35 @@ def tile_picked_route2_glusilu_e_kernel(tc, xT, gate, w1, w3, w2_words, w2_scale
         results = keep.tile([P, S], F32, name="results")
         hidden = {}
 
-        def gated_product(c, first=0, last=CHUNK):
-            if first == 0:
-                hidden[c] = keep.tile([P, CHUNK, PACK], BF16, name="hidden%d" % c, tag="h_words0" if c == 3 else "hidden%d" % c, align_bytes=64)
+        def gated_product(c, first=0, last=CHUNK, name=None, offset=None):
+            if name is not None:
+                shape = [P, CHUNK - first, PACK]
+                if offset is None:
+                    tile = keep.tile(shape, BF16, name=name, align_bytes=64)
+                else:
+                    tile = held.tile(shape, BF16, name=name, align_bytes=64, offset=offset)
+                hidden.setdefault(c, []).append((first, tile))
+            start, tile = hidden[c][-1]
             nc.vector.tensor_tensor(
-                hidden[c][:, first:last, :].rearrange("p c (r u) -> p c r u", u=2),
+                tile[:, first - start : last - start, :].rearrange("p c (r u) -> p c r u", u=2),
                 w3_banks[c][:, :, first:last].rearrange("p (r u) c -> p c r u", u=2),
                 silu_w1[:, c, :, first:last, :].rearrange("p r c u -> p c r u"),
                 MULT,
             )
 
         def second_layer(c):
-            words = keep.tile([P, CHUNK], U32, name="h_words%d" % c, tag="h_words%d" % c, align_bytes=64)
+            if c == 0:
+                words = held.tile([P, CHUNK], U32, name="h_words0", align_bytes=64, offset=HELD)
+            else:
+                words = keep.tile([P, CHUNK], U32, name="h_words%d" % c, align_bytes=64)
             scales = keep.tile([P, CHUNK], U8, name="h_scales%d" % c, tag="h_scales%d" % max(c - 1, 0), align_bytes=64)
-            nc.vector.quantize_mx(
-                out=words[:].bitcast(FP8X4), scales=scales[:], in_=hidden[c][:].rearrange("p c t -> p (c t)")
-            )
+            borders = [first for first, tile in hidden[c]] + [CHUNK]
+            for (first, tile), last in zip(hidden[c], borders[1:]):
+                nc.vector.quantize_mx(
+                    out=words[:, first:last].bitcast(FP8X4),
+                    scales=scales[:, first:last],
+                    in_=tile[:, 0 : last - first, :].rearrange("p c t -> p (c t)"),
+                )
             y_bank = psum.tile([P, CHUNK], F32, name="y_bank%d" % c, tag="w1_bank%d" % c)
             nc.tensor.matmul_mx(
                 out=y_bank[:],
@@ -261,16 +276,17 @@ def tile_picked_route2_glusilu_e_kernel(tc, xT, gate, w1, w3, w2_words, w2_scale
                 ACT.Copy,
             )
 
-        gated_product(0)
-        gated_product(1, 0, 64)
+        gated_product(0, name="hidden0")
+        gated_product(1, 0, 64, name="hidden1")
         y_banks = {0: second_layer(0)}
         gated_product(1, 64)
-        gated_product(2)
+        gated_product(2, 0, 64, name="hidden2")
         put(0, y_banks[0])
         y_banks[1] = second_layer(1)
-        gated_product(3)
-        y_banks[2] = second_layer(2)
+        gated_product(2, 64, name="hidden2_late", offset=HELD - 256)
+        gated_product(3, name="hidden3", offset=HELD + 256)
         put(1, y_banks[1])
+        y_banks[2] = second_layer(2)
         y_banks[3] = second_layer(3)
         put(2, y_banks[2])
         put(3, y_banks[3])

@@ -38,7 +38,8 @@ VECTOR_COLS = {
 
 CHUNK = 128
 CHUNKS = S // CHUNK
-HELD = 256
+OVERLAP = 256
+HALF_CHUNK = CHUNK // 2
 SCATTER_BORDERS = [0, 1, 2, CHUNKS]
 
 
@@ -180,7 +181,8 @@ def tile_picked_route2_glusilu_e_kernel(tc, xT, gate, w1, w3, w2_words, w2_scale
 
         def w1_pass(half, pair, u, g):
             tokens = slice(half * S // 2, (half + 1) * S // 2)
-            first_layer_pass(w1_banks[half, pair][:, u, :], W1, g, 2 * pair + u, tokens, (g, u) == (0, 0), (g, u) == (PASSES - 1, 1))
+            start, stop = (g, u) == (0, 0), (g, u) == (PASSES - 1, 1)
+            first_layer_pass(w1_banks[half, pair][:, u, :], W1, g, 2 * pair + u, tokens, start, stop)
 
         for pair in range(PAIRS):
             for u in range(2):
@@ -206,29 +208,29 @@ def tile_picked_route2_glusilu_e_kernel(tc, xT, gate, w1, w3, w2_words, w2_scale
 
         w3_banks = [psum.tile([P, PACK, CHUNK], F32, name="w3_bank%d" % c, tag="w3_bank%d" % c) for c in range(CHUNKS)]
 
-        def w3_pass(c, t, g, first=False, last=False):
-            first_layer_pass(w3_banks[c][:, t, :], W3, g, t, chunk_cols(c, c + 1), first, last)
-
         forward = [(t, g) for g in range(PASSES) for t in range(PACK)]
-        orders = [forward, forward[:PACK] + forward[: PACK - 1 : -1], forward[::-1], forward[::-1]]
-        for c in range(2):
-            for t, g in orders[c][:PACK]:
-                w3_pass(c, t, g, first=(t, g) == orders[c][0])
+        backward = forward[::-1]
+        orders = [forward, forward[:PACK] + backward[:PACK], backward, backward]
+        ahead = [PACK, PACK, 0, 0]
+
+        def w3_passes(c, steps):
+            for t, g in steps:
+                start, stop = (t, g) == orders[c][0], (t, g) == orders[c][-1]
+                first_layer_pass(w3_banks[c][:, t, :], W3, g, t, chunk_cols(c, c + 1), start, stop)
+
         for c in range(CHUNKS):
-            for t, g in orders[c][PACK if c < 2 else 0 :]:
-                w3_pass(c, t, g, first=(t, g) == orders[c][0], last=(t, g) == orders[c][-1])
+            w3_passes(c, orders[c][: ahead[c]])
+        for c in range(CHUNKS):
+            w3_passes(c, orders[c][ahead[c] :])
 
         results = keep.tile([P, S], F32, name="results")
-        hidden = {}
+        hidden = {c: [] for c in range(CHUNKS)}
 
-        def gated_product(c, first=0, last=CHUNK, name=None, offset=None):
-            if name is not None:
-                shape = [P, CHUNK - first, PACK]
-                if offset is None:
-                    tile = keep.tile(shape, BF16, name=name, align_bytes=64)
-                else:
-                    tile = held.tile(shape, BF16, name=name, align_bytes=64, offset=offset)
-                hidden.setdefault(c, []).append((first, tile))
+        def new_hidden(c, first, name, **place):
+            pool = held if place else keep
+            hidden[c].append((first, pool.tile([P, CHUNK - first, PACK], BF16, name=name, align_bytes=64, **place)))
+
+        def gated_product(c, first=0, last=CHUNK):
             start, tile = hidden[c][-1]
             nc.vector.tensor_tensor(
                 tile[:, first - start : last - start, :].rearrange("p c (r u) -> p c r u", u=2),
@@ -239,10 +241,10 @@ def tile_picked_route2_glusilu_e_kernel(tc, xT, gate, w1, w3, w2_words, w2_scale
 
         def second_layer(c):
             if c == 0:
-                words = held.tile([P, CHUNK], U32, name="h_words0", align_bytes=64, offset=HELD)
+                words = held.tile([P, CHUNK], U32, name="h_words0", align_bytes=64, offset=OVERLAP)
             else:
                 words = keep.tile([P, CHUNK], U32, name="h_words%d" % c, align_bytes=64)
-            scales = keep.tile([P, CHUNK], U8, name="h_scales%d" % c, tag="h_scales%d" % max(c - 1, 0), align_bytes=64)
+            scales = keep.tile([P, CHUNK], U8, name="h_scales%d" % c, align_bytes=64)
             borders = [first for first, tile in hidden[c]] + [CHUNK]
             for (first, tile), last in zip(hidden[c], borders[1:]):
                 nc.vector.quantize_mx(
@@ -276,15 +278,20 @@ def tile_picked_route2_glusilu_e_kernel(tc, xT, gate, w1, w3, w2_words, w2_scale
                 ACT.Copy,
             )
 
-        gated_product(0, name="hidden0")
-        gated_product(1, 0, 64, name="hidden1")
+        new_hidden(0, 0, "hidden0")
+        gated_product(0)
+        new_hidden(1, 0, "hidden1")
+        gated_product(1, 0, HALF_CHUNK)
         y_banks = {0: second_layer(0)}
-        gated_product(1, 64)
-        gated_product(2, 0, 64, name="hidden2")
-        put(0, y_banks[0])
+        gated_product(1, HALF_CHUNK)
+        new_hidden(2, 0, "hidden2")
+        gated_product(2, 0, HALF_CHUNK)
         y_banks[1] = second_layer(1)
-        gated_product(2, 64, name="hidden2_late", offset=HELD - 256)
-        gated_product(3, name="hidden3", offset=HELD + 256)
+        put(0, y_banks[0])
+        new_hidden(2, HALF_CHUNK, "hidden2_late", offset=0)
+        gated_product(2, HALF_CHUNK)
+        new_hidden(3, 0, "hidden3", offset=2 * OVERLAP)
+        gated_product(3)
         put(1, y_banks[1])
         y_banks[2] = second_layer(2)
         y_banks[3] = second_layer(3)

@@ -40,7 +40,8 @@ CHUNK = 128
 CHUNKS = S // CHUNK
 OVERLAP = 256
 HALF_CHUNK = CHUNK // 2
-SCATTER_BORDERS = [0, 1, 2, CHUNKS]
+PIECES = [0, 128, 320, 512]
+GATE_CUT = 320
 
 
 def tile_picked_route2_glusilu_e_kernel(tc, xT, gate, w1, w3, w2_words, w2_scales, offs, dst, out):
@@ -90,12 +91,12 @@ def tile_picked_route2_glusilu_e_kernel(tc, xT, gate, w1, w3, w2_words, w2_scale
             for g in range(PASSES):
                 w_raw[mat, g] = load_pass((w1, w3)[mat], g, "w_raw%d%d" % (mat, g))
         gates = keep.tile([P, S], F32, name="gates")
-        nc.sync.dma_start(gates[:, 0 : S // 2], gate[:, 0 : S // 2])
+        nc.sync.dma_start(gates[:, 0:GATE_CUT], gate[:, 0:GATE_CUT])
         w2_codes = keep.tile([P, 2 * N], U8, name="w2_codes", align_bytes=64)
         nc.sync.dma_start(w2_codes[:].bitcast(I32), w2_words[0].bitcast(I32))
         places = keep.tile([P, S // LIST_ROWS], U16, name="places")
         nc.sync.dma_start(places[:], dst)
-        nc.sync.dma_start(gates[:, S // 2 : S], gate[:, S // 2 : S])
+        nc.sync.dma_start(gates[:, GATE_CUT:S], gate[:, GATE_CUT:S])
 
         x_words = [keep.tile([P, T], U32, name="x_words%d" % g, align_bytes=64) for g in range(PASSES)]
         picked_words = [keep.tile([P, S], U32, name="picked_words%d" % g, align_bytes=64) for g in range(PASSES)]
@@ -224,78 +225,95 @@ def tile_picked_route2_glusilu_e_kernel(tc, xT, gate, w1, w3, w2_words, w2_scale
             w3_passes(c, orders[c][ahead[c] :])
 
         results = keep.tile([P, S], F32, name="results")
-        hidden = {c: [] for c in range(CHUNKS)}
+        hidden = {}
+        h_words, h_scales, y_banks = {}, {}, {}
 
-        def new_hidden(c, first, name, **place):
-            pool = held if place else keep
-            hidden[c].append((first, pool.tile([P, CHUNK - first, PACK], BF16, name=name, align_bytes=64, **place)))
+        def held_tile(shape, dtype, name, offset):
+            if offset is None:
+                return keep.tile(shape, dtype, name=name, align_bytes=64)
+            return held.tile(shape, dtype, name=name, align_bytes=64, offset=offset)
 
-        def gated_product(c, first=0, last=CHUNK):
-            start, tile = hidden[c][-1]
+        def new_piece(k, offset=None):
+            tokens = PIECES[k + 1] - PIECES[k]
+            width = -(-tokens // CHUNK) * CHUNK
+            h_words[k] = held_tile([P, width], I32, "h_words%d" % k, offset)
+            h_scales[k] = keep.tile([P, width], U8, name="h_scales%d" % k, align_bytes=64)
+            if tokens < width:
+                nc.vector.memset(h_words[k][:, tokens:width], 0)
+                nc.vector.memset(h_scales[k][:, tokens:width].bitcast(I32), 0)
+
+        def new_hidden(first, end, offset=None):
+            hidden[first] = (end, held_tile([P, end - first, PACK], BF16, "hidden%d" % first, offset))
+
+        def hidden_cols(first, end):
+            start = max(s for s in hidden if s <= first)
+            return hidden[start][1][:, first - start : end - start, :]
+
+        def gated_product(first, end):
+            c, lo, hi = first // CHUNK, first % CHUNK, (end - 1) % CHUNK + 1
             nc.vector.tensor_tensor(
-                tile[:, first - start : last - start, :].rearrange("p c (r u) -> p c r u", u=2),
-                w3_banks[c][:, :, first:last].rearrange("p (r u) c -> p c r u", u=2),
-                silu_w1[:, c, :, first:last, :].rearrange("p r c u -> p c r u"),
+                hidden_cols(first, end).rearrange("p c (r u) -> p c r u", u=2),
+                w3_banks[c][:, :, lo:hi].rearrange("p (r u) c -> p c r u", u=2),
+                silu_w1[:, c, :, lo:hi, :].rearrange("p r c u -> p c r u"),
                 MULT,
             )
 
-        def second_layer(c):
-            if c == 0:
-                words = held.tile([P, CHUNK], U32, name="h_words0", align_bytes=64, offset=OVERLAP)
-            else:
-                words = keep.tile([P, CHUNK], U32, name="h_words%d" % c, align_bytes=64)
-            scales = keep.tile([P, CHUNK], U8, name="h_scales%d" % c, align_bytes=64)
-            borders = [first for first, tile in hidden[c]] + [CHUNK]
-            for (first, tile), last in zip(hidden[c], borders[1:]):
-                nc.vector.quantize_mx(
-                    out=words[:, first:last].bitcast(FP8X4),
-                    scales=scales[:, first:last],
-                    in_=tile[:, 0 : last - first, :].rearrange("p c t -> p (c t)"),
-                )
-            y_bank = psum.tile([P, CHUNK], F32, name="y_bank%d" % c, tag="w1_bank%d" % c)
+        def quantise_hidden(first, end):
+            k = max(i for i in range(len(PIECES) - 1) if PIECES[i] <= first)
+            cols = slice(first - PIECES[k], end - PIECES[k])
+            nc.vector.quantize_mx(
+                out=h_words[k][:, cols].bitcast(FP8X4),
+                scales=h_scales[k][:, cols],
+                in_=hidden_cols(first, end).rearrange("p c t -> p (c t)"),
+            )
+
+        def second_layer(k):
+            width = h_words[k].shape[1]
+            y_banks[k] = psum.tile([P, width], F32, name="y_bank%d" % k, tag="w1_bank%d" % k)
             nc.tensor.matmul_mx(
-                out=y_bank[:],
+                out=y_banks[k][:],
                 lhsT=w2_codes[:].bitcast(FP4X4),
                 lhsT_scale=w2_plane[:],
-                rhs=words[:].bitcast(FP8X4),
-                rhs_scale=scales[:],
+                rhs=h_words[k][:].bitcast(FP8X4),
+                rhs_scale=h_scales[k][:],
                 start=True,
                 stop=True,
             )
-            return y_bank
 
-        def put(c, y_bank):
-            cols = chunk_cols(c, c + 1)
-            nc.vector.tensor_tensor(results[:, cols], y_bank[:], gates[:, cols], MULT)
-            if c + 1 in SCATTER_BORDERS:
-                scatter(SCATTER_BORDERS[SCATTER_BORDERS.index(c + 1) - 1], c + 1)
-
-        def scatter(c0, c1):
-            cols = chunk_cols(c0, c1)
+        def put(k):
+            first, end = PIECES[k], PIECES[k + 1]
+            nc.vector.tensor_tensor(results[:, first:end], y_banks[k][:, 0 : end - first], gates[:, first:end], MULT)
             nc.scalar.activation(
-                window[:].indirect(places[:, cols.start // LIST_ROWS : cols.stop // LIST_ROWS]),
-                results[:, cols],
-                ACT.Copy,
+                window[:].indirect(places[:, first // LIST_ROWS : end // LIST_ROWS]), results[:, first:end], ACT.Copy
             )
 
-        new_hidden(0, 0, "hidden0")
-        gated_product(0)
-        new_hidden(1, 0, "hidden1")
-        gated_product(1, 0, HALF_CHUNK)
-        y_banks = {0: second_layer(0)}
-        gated_product(1, HALF_CHUNK)
-        new_hidden(2, 0, "hidden2")
-        gated_product(2, 0, HALF_CHUNK)
-        y_banks[1] = second_layer(1)
-        put(0, y_banks[0])
-        new_hidden(2, HALF_CHUNK, "hidden2_late", offset=0)
-        gated_product(2, HALF_CHUNK)
-        new_hidden(3, 0, "hidden3", offset=2 * OVERLAP)
-        gated_product(3)
-        put(1, y_banks[1])
-        y_banks[2] = second_layer(2)
-        y_banks[3] = second_layer(3)
-        put(2, y_banks[2])
-        put(3, y_banks[3])
+        new_piece(0, offset=256)
+        new_piece(1, offset=1024)
+        new_piece(2)
+        new_hidden(0, 128)
+        gated_product(0, 128)
+        new_hidden(128, 256)
+        gated_product(128, 192)
+        quantise_hidden(0, 128)
+        second_layer(0)
+        gated_product(192, 256)
+        new_hidden(256, 320)
+        gated_product(256, 320)
+        quantise_hidden(128, 256)
+        put(0)
+        quantise_hidden(256, 320)
+        second_layer(1)
+        new_hidden(320, 384, offset=0)
+        gated_product(320, 384)
+        new_hidden(384, 448, offset=512)
+        gated_product(384, 448)
+        quantise_hidden(320, 384)
+        put(1)
+        new_hidden(448, 512, offset=1024)
+        gated_product(448, 512)
+        quantise_hidden(384, 448)
+        quantise_hidden(448, 512)
+        second_layer(2)
+        put(2)
 
         nc.sync.dma_start(out, window[:])

@@ -33,7 +33,7 @@ VECTOR_COLS = {
     (W1, 0): slice(208, 256),
     (W1, 1): slice(160, 256),
     (W3, 0): slice(128, 256),
-    (W3, 1): slice(0, 160),
+    (W3, 1): slice(40, 192),
 }
 
 CHUNK = 128
@@ -53,7 +53,7 @@ def tile_picked_route2_glusilu_e_kernel(tc, xT, gate, w1, w3, w2_words, w2_scale
         psum = ctx.enter_context(tc.psum_pool(name="psum", bufs=1))
 
         def load_pass(src, g, name):
-            raw = keep.tile([P, PACK, src.shape[1]], F32, name=name, tag=name)
+            raw = keep.tile([P, PACK, src.shape[1]], F32, name=name, tag=name, align_bytes=64)
             rows = src[g * K_PASS : (g + 1) * K_PASS, :].rearrange("(p j) c -> p j c", j=PACK)
             nc.sync.dma_start(out=raw[:], in_=rows)
             return raw
@@ -99,7 +99,6 @@ def tile_picked_route2_glusilu_e_kernel(tc, xT, gate, w1, w3, w2_words, w2_scale
         nc.sync.dma_start(gates[:, GATE_CUT:S], gate[:, GATE_CUT:S])
 
         x_words = [keep.tile([P, T], U32, name="x_words%d" % g, align_bytes=64) for g in range(PASSES)]
-        picked_words = [keep.tile([P, S], U32, name="picked_words%d" % g, align_bytes=64) for g in range(PASSES)]
         picked_scales = keep.tile([P, S], U8, name="picked_scales", align_bytes=64)
 
         def quantise_tokens(g):
@@ -125,41 +124,53 @@ def tile_picked_route2_glusilu_e_kernel(tc, xT, gate, w1, w3, w2_words, w2_scale
         def pick(picked, table):
             nc.vector.tensor_copy(picked[:], table[:].indirect(offsets[:]))
 
+        picked_words = {}
+
+        def pick_words(g, tag):
+            picked_words[g] = keep.tile([P, S], U32, name="picked_words%d" % g, tag=tag, align_bytes=64)
+            pick(picked_words[g], x_words[g])
+
         w_rounded, w_words, w_scales = {}, {}, {}
 
         def round_weights(mat, g):
             vector_cols = VECTOR_COLS[mat, g]
             dealt = w_raw[mat, g][:].rearrange("p j (m t) -> p m j t", t=PACK)
-            rounded = keep.tile([P, PACK, P, PACK], BF16, name="w_bf%d%d" % (mat, g), align_bytes=64)
-            w_rounded[mat, g] = rounded
             for pair in range(PAIRS):
+                name = "w_bf%d%d%d" % (mat, g, pair)
+                rounded = keep.tile([P, 2, P, PACK], BF16, name=name, tag=name, align_bytes=64)
+                w_rounded[mat, g, pair] = rounded
                 lo = min(max(vector_cols.start - pair * P, 0), P)
                 hi = min(max(vector_cols.stop - pair * P, 0), P)
                 for round_on, m0, m1 in ((round_on_scalar, 0, lo), (round_on_vector, lo, hi), (round_on_scalar, hi, P)):
                     if m1 > m0:
                         round_on(
-                            rounded[:, 2 * pair : 2 * pair + 2, m0:m1, :].rearrange("p u m j -> p m j u"),
+                            rounded[:, :, m0:m1, :].rearrange("p u m j -> p m j u"),
                             dealt[:, m0:m1, :, 2 * pair : 2 * pair + 2],
                         )
 
-        def quantise_weights(mat, g, borders):
-            words = keep.tile([P, H], U32, name="w_words%d%d" % (mat, g), align_bytes=64)
-            scales = keep.tile([P, H], U8, name="w_scales%d%d" % (mat, g), align_bytes=64)
-            w_words[mat, g], w_scales[mat, g] = words, scales
-            for first, last in zip(borders, borders[1:]):
-                cols = slice(first * P, last * P)
+        def quantise_weights(mat, g, spans):
+            if (mat, g) not in w_words:
+                w_words[mat, g] = keep.tile([P, H], U32, name="w_words%d%d" % (mat, g), align_bytes=64)
+                w_scales[mat, g] = keep.tile([P, H], U8, name="w_scales%d%d" % (mat, g), align_bytes=64)
+            words, scales = w_words[mat, g], w_scales[mat, g]
+            for first, last in spans:
+                cols = slice(first, last)
+                pair, start = divmod(first, 2 * P)
+                rounded = w_rounded[mat, g, pair][:].rearrange("p u m j -> p (u m j)")
                 nc.vector.quantize_mx(
                     out=words[:, cols].bitcast(FP8X4),
                     scales=scales[:, cols],
-                    in_=w_rounded[mat, g][:, first:last, :, :].rearrange("p t m j -> p (t m j)"),
+                    in_=rounded[:, start * PACK : (start + last - first) * PACK],
                 )
 
+        by_pairs = [(2 * P * pair, 2 * P * (pair + 1)) for pair in range(PAIRS)]
         quantise_tokens(0)
-        pick(picked_words[0], x_words[0])
+        pick_words(0, "picked_words0")
         quantise_tokens(1)
         round_weights(W1, 0)
         pick(picked_scales, x_scales)
-        pick(picked_words[1], x_words[1])
+        quantise_weights(W1, 0, by_pairs[:1])
+        pick_words(1, "w_raw%d%d" % (W1, 0))
 
         def first_layer_pass(acc, mat, g, t, tokens, start, stop):
             cols = slice(t * P, (t + 1) * P)
@@ -173,7 +184,7 @@ def tile_picked_route2_glusilu_e_kernel(tc, xT, gate, w1, w3, w2_words, w2_scale
                 stop=stop,
             )
 
-        quantise_weights(W1, 0, (0, PACK))
+        quantise_weights(W1, 0, by_pairs[1:])
         w1_banks = {}
         for half in range(2):
             for pair in range(PAIRS):
@@ -190,29 +201,37 @@ def tile_picked_route2_glusilu_e_kernel(tc, xT, gate, w1, w3, w2_words, w2_scale
                 for half in range(2):
                     w1_pass(half, pair, u, 0)
         round_weights(W1, 1)
-        quantise_weights(W1, 1, (0, 2, PACK))
+        quantise_weights(W1, 1, by_pairs)
         for half in range(2):
             for pair in range(PAIRS):
                 for u in range(2):
                     w1_pass(half, pair, u, 1)
 
         round_weights(W3, 0)
-        quantise_weights(W3, 0, (0, 2, PACK))
-        round_weights(W3, 1)
-        quantise_weights(W3, 1, (0, 2, 3, PACK))
+        quantise_weights(W3, 0, by_pairs)
+        silu_w1 = {}
 
-        silu_w1 = keep.tile([P, CHUNKS, PAIRS, CHUNK, 2], F32, name="silu_w1", tag="w_raw%d%d" % (W3, PASSES - 1))
-        for c in range(CHUNKS):
+        def silu(c, values):
+            silu_w1[c] = values
             for pair in range(PAIRS):
                 sums = w1_banks[c // 2, pair][:, :, chunk_cols(c % 2, c % 2 + 1)]
-                nc.scalar.activation(silu_w1[:, c, pair, :, :], sums.rearrange("p u c -> p c u"), ACT.Silu)
+                nc.scalar.activation(values[:, pair, :, :], sums.rearrange("p u c -> p c u"), ACT.Silu)
+
+        silu(0, keep.tile([P, PAIRS, CHUNK, 2], F32, name="silu_first", tag="w_raw%d%d" % (W3, 0), align_bytes=64)[:])
+        round_weights(W3, 1)
+        halves = [(t * P + lo, t * P + lo + P // 2) for lo in (0, P // 2) for t in (2, 3)]
+        quantise_weights(W3, 1, by_pairs[:1] + halves)
+
+        last_raw = "w_raw%d%d" % (W3, PASSES - 1)
+        silu_rest = keep.tile([P, CHUNKS - 1, PAIRS, CHUNK, 2], F32, name="silu_rest", tag=last_raw, align_bytes=64)
+        for c in range(1, CHUNKS):
+            silu(c, silu_rest[:, c - 1, :, :, :])
 
         w3_banks = [psum.tile([P, PACK, CHUNK], F32, name="w3_bank%d" % c, tag="w3_bank%d" % c) for c in range(CHUNKS)]
 
         forward = [(t, g) for g in range(PASSES) for t in range(PACK)]
         backward = forward[::-1]
-        orders = [forward, forward[:PACK] + backward[:PACK], backward, backward]
-        ahead = [PACK, PACK, 0, 0]
+        orders = [forward] + [forward[:PACK] + backward[:PACK]] * (CHUNKS - 1)
 
         def w3_passes(c, steps):
             for t, g in steps:
@@ -220,9 +239,9 @@ def tile_picked_route2_glusilu_e_kernel(tc, xT, gate, w1, w3, w2_words, w2_scale
                 first_layer_pass(w3_banks[c][:, t, :], W3, g, t, chunk_cols(c, c + 1), start, stop)
 
         for c in range(CHUNKS):
-            w3_passes(c, orders[c][: ahead[c]])
+            w3_passes(c, orders[c][:PACK])
         for c in range(CHUNKS):
-            w3_passes(c, orders[c][ahead[c] :])
+            w3_passes(c, orders[c][PACK:])
 
         results = keep.tile([P, S], F32, name="results")
         hidden = {}
@@ -254,7 +273,7 @@ def tile_picked_route2_glusilu_e_kernel(tc, xT, gate, w1, w3, w2_words, w2_scale
             nc.vector.tensor_tensor(
                 hidden_cols(first, end).rearrange("p c (r u) -> p c r u", u=2),
                 w3_banks[c][:, :, lo:hi].rearrange("p (r u) c -> p c r u", u=2),
-                silu_w1[:, c, :, lo:hi, :].rearrange("p r c u -> p c r u"),
+                silu_w1[c][:, :, lo:hi, :].rearrange("p r c u -> p c r u"),
                 MULT,
             )
 
@@ -267,15 +286,17 @@ def tile_picked_route2_glusilu_e_kernel(tc, xT, gate, w1, w3, w2_words, w2_scale
                 in_=hidden_cols(first, end).rearrange("p c t -> p (c t)"),
             )
 
-        def second_layer(k):
-            width = h_words[k].shape[1]
-            y_banks[k] = psum.tile([P, width], F32, name="y_bank%d" % k, tag="w1_bank%d" % k)
+        def second_layer(k, block):
+            if block == 0:
+                width = h_words[k].shape[1]
+                y_banks[k] = psum.tile([P, width], F32, name="y_bank%d" % k, tag="w1_bank%d" % k)
+            cols = chunk_cols(block, block + 1)
             nc.tensor.matmul_mx(
-                out=y_banks[k][:],
+                out=y_banks[k][:, cols],
                 lhsT=w2_codes[:].bitcast(FP4X4),
                 lhsT_scale=w2_plane[:],
-                rhs=h_words[k][:].bitcast(FP8X4),
-                rhs_scale=h_scales[k][:],
+                rhs=h_words[k][:, cols].bitcast(FP8X4),
+                rhs_scale=h_scales[k][:, cols],
                 start=True,
                 stop=True,
             )
@@ -288,32 +309,30 @@ def tile_picked_route2_glusilu_e_kernel(tc, xT, gate, w1, w3, w2_words, w2_scale
             )
 
         new_piece(0, offset=256)
-        new_piece(1, offset=1024)
+        new_piece(1)
         new_piece(2)
         new_hidden(0, 128)
         gated_product(0, 128)
         new_hidden(128, 256)
         gated_product(128, 192)
         quantise_hidden(0, 128)
-        second_layer(0)
+        second_layer(0, 0)
         gated_product(192, 256)
         new_hidden(256, 320)
         gated_product(256, 320)
         quantise_hidden(128, 256)
+        second_layer(1, 0)
         put(0)
         quantise_hidden(256, 320)
-        second_layer(1)
-        new_hidden(320, 384, offset=0)
+        second_layer(1, 1)
+        new_hidden(320, 512, offset=0)
         gated_product(320, 384)
-        new_hidden(384, 448, offset=512)
-        gated_product(384, 448)
-        quantise_hidden(320, 384)
+        gated_product(384, 512)
         put(1)
-        new_hidden(448, 512, offset=1024)
-        gated_product(448, 512)
-        quantise_hidden(384, 448)
+        quantise_hidden(320, 448)
+        second_layer(2, 0)
         quantise_hidden(448, 512)
-        second_layer(2)
+        second_layer(2, 1)
         put(2)
 
         nc.sync.dma_start(out, window[:])

@@ -252,14 +252,16 @@ def tile_picked_route2_glusilu_e_kernel(tc, xT, gate, w1, w3, w2_words, w2_scale
                 return keep.tile(shape, dtype, name=name, align_bytes=64)
             return held.tile(shape, dtype, name=name, align_bytes=64, offset=offset)
 
-        def new_piece(k, offset=None):
-            tokens = PIECES[k + 1] - PIECES[k]
-            width = -(-tokens // CHUNK) * CHUNK
-            h_words[k] = held_tile([P, width], I32, "h_words%d" % k, offset)
-            h_scales[k] = keep.tile([P, width], U8, name="h_scales%d" % k, align_bytes=64)
-            if tokens < width:
-                nc.vector.memset(h_words[k][:, tokens:width], 0)
-                nc.vector.memset(h_scales[k][:, tokens:width].bitcast(I32), 0)
+        def new_block(k, block, offset=None, scale_tag=None):
+            tokens = min(PIECES[k + 1] - PIECES[k] - block * CHUNK, CHUNK)
+            name = "%d_%d" % (k, block)
+            words = held_tile([P, CHUNK], I32, "h_words" + name, offset)
+            tag = scale_tag or "h_scales" + name
+            scales = keep.tile([P, CHUNK], U8, name="h_scales" + name, tag=tag, align_bytes=64)
+            h_words[k, block], h_scales[k, block] = words, scales
+            if tokens < CHUNK:
+                nc.vector.memset(words[:, tokens:CHUNK], 0)
+                nc.vector.memset(scales[:, tokens:CHUNK].bitcast(I32), 0)
 
         def new_hidden(first, end, offset=None):
             hidden[first] = (end, held_tile([P, end - first, PACK], BF16, "hidden%d" % first, offset))
@@ -279,24 +281,25 @@ def tile_picked_route2_glusilu_e_kernel(tc, xT, gate, w1, w3, w2_words, w2_scale
 
         def quantise_hidden(first, end):
             k = max(i for i in range(len(PIECES) - 1) if PIECES[i] <= first)
-            cols = slice(first - PIECES[k], end - PIECES[k])
+            block, start = divmod(first - PIECES[k], CHUNK)
+            cols = slice(start, start + end - first)
             nc.vector.quantize_mx(
-                out=h_words[k][:, cols].bitcast(FP8X4),
-                scales=h_scales[k][:, cols],
+                out=h_words[k, block][:, cols].bitcast(FP8X4),
+                scales=h_scales[k, block][:, cols],
                 in_=hidden_cols(first, end).rearrange("p c t -> p (c t)"),
             )
 
         def second_layer(k, block):
             if block == 0:
-                width = h_words[k].shape[1]
+                width = -(-(PIECES[k + 1] - PIECES[k]) // CHUNK) * CHUNK
                 y_banks[k] = psum.tile([P, width], F32, name="y_bank%d" % k, tag="w1_bank%d" % k)
             cols = chunk_cols(block, block + 1)
             nc.tensor.matmul_mx(
                 out=y_banks[k][:, cols],
                 lhsT=w2_codes[:].bitcast(FP4X4),
                 lhsT_scale=w2_plane[:],
-                rhs=h_words[k][:, cols].bitcast(FP8X4),
-                rhs_scale=h_scales[k][:, cols],
+                rhs=h_words[k, block][:].bitcast(FP8X4),
+                rhs_scale=h_scales[k, block][:],
                 start=True,
                 stop=True,
             )
@@ -308,9 +311,10 @@ def tile_picked_route2_glusilu_e_kernel(tc, xT, gate, w1, w3, w2_words, w2_scale
                 window[:].indirect(places[:, first // LIST_ROWS : end // LIST_ROWS]), results[:, first:end], ACT.Copy
             )
 
-        new_piece(0, offset=256)
-        new_piece(1)
-        new_piece(2)
+        new_block(0, 0, offset=256)
+        new_block(1, 1)
+        new_block(2, 0)
+        new_block(2, 1)
         new_hidden(0, 128)
         gated_product(0, 128)
         new_hidden(128, 256)
@@ -320,15 +324,17 @@ def tile_picked_route2_glusilu_e_kernel(tc, xT, gate, w1, w3, w2_words, w2_scale
         gated_product(192, 256)
         new_hidden(256, 320)
         gated_product(256, 320)
+        put(0)
+        new_block(1, 0, scale_tag="h_scales0_0")
         quantise_hidden(128, 256)
         second_layer(1, 0)
-        put(0)
         quantise_hidden(256, 320)
         second_layer(1, 1)
         new_hidden(320, 512, offset=0)
         gated_product(320, 384)
-        gated_product(384, 512)
+        gated_product(384, 448)
         put(1)
+        gated_product(448, 512)
         quantise_hidden(320, 448)
         second_layer(2, 0)
         quantise_hidden(448, 512)

@@ -312,6 +312,7 @@ def tile_picked_route2_glusilu_e_kernel(tc, xT, gate, w1, w3, w2_words, w2_scale
             )
 
         new_block(0, 0, offset=256)
+        new_block(1, 0)
         new_block(1, 1)
         new_block(2, 0)
         new_block(2, 1)
@@ -324,17 +325,16 @@ def tile_picked_route2_glusilu_e_kernel(tc, xT, gate, w1, w3, w2_words, w2_scale
         gated_product(192, 256)
         new_hidden(256, 320)
         gated_product(256, 320)
-        put(0)
-        new_block(1, 0, scale_tag="h_scales0_0")
         quantise_hidden(128, 256)
         second_layer(1, 0)
+        put(0)
         quantise_hidden(256, 320)
         second_layer(1, 1)
         new_hidden(320, 512, offset=0)
         gated_product(320, 384)
-        gated_product(384, 448)
+        gated_product(384, 480)
         put(1)
-        gated_product(448, 512)
+        gated_product(480, 512)
         quantise_hidden(320, 448)
         second_layer(2, 0)
         quantise_hidden(448, 512)

@@ -215,15 +215,17 @@ def tile_picked_route2_glusilu_e_kernel(tc, xT, gate, w1, w3, w2_words, w2_scale
             silu_w1[c] = values
             for pair in range(PAIRS):
                 sums = w1_banks[c // 2, pair][:, :, chunk_cols(c % 2, c % 2 + 1)]
-                nc.scalar.activation(values[:, pair, :, :], sums.rearrange("p u c -> p c u"), ACT.Silu)
+                nc.scalar.activation(
+                    values[:, :, 2 * pair : 2 * pair + 2, :], sums.rearrange("p u (c i) -> p c u i", i=2), ACT.Silu
+                )
 
-        silu(0, keep.tile([P, PAIRS, CHUNK, 2], F32, name="silu_first", tag="w_raw%d%d" % (W3, 0), align_bytes=64)[:])
+        silu(0, keep.tile([P, CHUNK // 2, PACK, 2], F32, name="silu_first", tag="w_raw%d%d" % (W3, 0), align_bytes=64)[:])
         round_weights(W3, 1)
         halves = [(t * P + lo, t * P + lo + P // 2) for lo in (0, P // 2) for t in (2, 3)]
         quantise_weights(W3, 1, by_pairs[:1] + halves)
 
         last_raw = "w_raw%d%d" % (W3, PASSES - 1)
-        silu_rest = keep.tile([P, CHUNKS - 1, PAIRS, CHUNK, 2], F32, name="silu_rest", tag=last_raw, align_bytes=64)
+        silu_rest = keep.tile([P, CHUNKS - 1, CHUNK // 2, PACK, 2], F32, name="silu_rest", tag=last_raw, align_bytes=64)
         for c in range(1, CHUNKS):
             silu(c, silu_rest[:, c - 1, :, :, :])
 
@@ -273,9 +275,9 @@ def tile_picked_route2_glusilu_e_kernel(tc, xT, gate, w1, w3, w2_words, w2_scale
         def gated_product(first, end):
             c, lo, hi = first // CHUNK, first % CHUNK, (end - 1) % CHUNK + 1
             nc.vector.tensor_tensor(
-                hidden_cols(first, end).rearrange("p c (r u) -> p c r u", u=2),
-                w3_banks[c][:, :, lo:hi].rearrange("p (r u) c -> p c r u", u=2),
-                silu_w1[c][:, :, lo:hi, :].rearrange("p r c u -> p c r u"),
+                hidden_cols(first, end).rearrange("p (c i) t -> p c t i", i=2),
+                w3_banks[c][:, :, lo:hi].rearrange("p t (c i) -> p c t i", i=2),
+                silu_w1[c][:, lo // 2 : hi // 2, :, :],
                 MULT,
             )
 

from contextlib import ExitStack

import concourse.mybir as mybir

K, T, S, H, N, U = 1024, 1024, 512, 512, 128, 1024
FLOPS = 2 * S * (2 * K * H + H * N)

F32 = mybir.dt.float32
BF16 = mybir.dt.bfloat16
I32 = mybir.dt.int32
U32 = mybir.dt.uint32
U16 = mybir.dt.uint16
U8 = mybir.dt.uint8
FP8X4 = mybir.dt.float8_e4m3fn_x4
FP4X4 = mybir.dt.float4_e2m1fn_x4
ACT = mybir.ActivationFunctionType
MULT = mybir.AluOpType.mult

P = 128
PACK = 4
K_PASS = P * PACK
PASSES = K // K_PASS
LIST_ROWS = 16
SCALE_ROWS = 4
LINE = 4
W1, W3 = 0, 1

QUADRANT = 32
PAIRS = 2

VECTOR_TOKENS = 544
VECTOR_COLS = {
    (W1, 0): slice(208, 256),
    (W1, 1): slice(160, 256),
    (W3, 0): slice(128, 256),
    (W3, 1): slice(40, 192),
}

CHUNK = 128
CHUNKS = S // CHUNK
OVERLAP = 256
HALF_CHUNK = CHUNK // 2
PIECES = [0, 128, 320, 512]
GATE_CUT = 320


def tile_picked_route2_glusilu_e_kernel(tc, xT, gate, w1, w3, w2_words, w2_scales, offs, dst, out):
    nc = tc.nc

    with ExitStack() as ctx:
        keep = ctx.enter_context(tc.tile_pool(name="keep", bufs=1))
        held = ctx.enter_context(tc.tile_pool(name="held", bufs=1))
        psum = ctx.enter_context(tc.psum_pool(name="psum", bufs=1))

        def load_pass(src, g, name):
            raw = keep.tile([P, PACK, src.shape[1]], F32, name=name, tag=name, align_bytes=64)
            rows = src[g * K_PASS : (g + 1) * K_PASS, :].rearrange("(p j) c -> p j c", j=PACK)
            nc.sync.dma_start(out=raw[:], in_=rows)
            return raw

        def chunk_cols(c0, c1, per_token=1):
            return slice(c0 * CHUNK * per_token, c1 * CHUNK * per_token)

        def round_on_scalar(rounded, raw):
            nc.scalar.activation(rounded, raw, ACT.Copy)

        def round_on_vector(rounded, raw):
            nc.vector.tensor_copy(rounded, raw)

        window = keep.tile([P, U], F32, name="window")
        nc.vector.memset(window[:], 0.0)
        x_scales = keep.tile([P, T], U8, name="x_scales", align_bytes=64)
        nc.vector.memset(x_scales[:].bitcast(I32), 0)
        w2_plane = keep.tile([P, N], U8, name="w2_plane", align_bytes=64)
        nc.gpsimd.memset(w2_plane[:].bitcast(I32), 0)
        for q in range(P // QUADRANT):
            nc.scalar.dma_start(
                w2_plane[QUADRANT * q : QUADRANT * q + SCALE_ROWS, :].bitcast(I32),
                w2_scales[0, SCALE_ROWS * q : SCALE_ROWS * (q + 1), :].bitcast(I32),
            )

        warm = keep.tile([P, 8], F32, name="warm")
        nc.scalar.activation(warm[:], window[:, 0:8], ACT.Silu)

        x_raw = {0: load_pass(xT, 0, "x_raw0")}
        offsets = keep.tile([P, S // LIST_ROWS], U16, name="offsets")
        nc.sync.dma_start(offsets[:], offs)
        x_raw[1] = load_pass(xT, 1, "x_raw1")
        w_raw = {}
        for mat in (W1, W3):
            for g in range(PASSES):
                w_raw[mat, g] = load_pass((w1, w3)[mat], g, "w_raw%d%d" % (mat, g))
        gates = keep.tile([P, S], F32, name="gates")
        nc.sync.dma_start(gates[:, 0:GATE_CUT], gate[:, 0:GATE_CUT])
        w2_codes = keep.tile([P, 2 * N], U8, name="w2_codes", align_bytes=64)
        nc.sync.dma_start(w2_codes[:].bitcast(I32), w2_words[0].bitcast(I32))
        places = keep.tile([P, S // LIST_ROWS], U16, name="places")
        nc.sync.dma_start(places[:], dst)
        nc.sync.dma_start(gates[:, GATE_CUT:S], gate[:, GATE_CUT:S])

        x_words = [keep.tile([P, T], U32, name="x_words%d" % g, align_bytes=64) for g in range(PASSES)]
        picked_scales = keep.tile([P, S], U8, name="picked_scales", align_bytes=64)

        def quantise_tokens(g):
            rounded = keep.tile([P, T * PACK], BF16, name="x_bf%d" % g, align_bytes=64)
            middle, last_quarter = T // 2, 3 * T // 4
            for round_on, c0, c1 in (
                (round_on_scalar, VECTOR_TOKENS, last_quarter),
                (round_on_scalar, last_quarter, T),
                (round_on_vector, 0, middle),
                (round_on_vector, middle, VECTOR_TOKENS),
            ):
                round_on(
                    rounded[:, c0 * PACK : c1 * PACK].rearrange("p (c i j) -> p c j i", i=LINE, j=PACK),
                    x_raw[g][:, :, c0:c1].rearrange("p j (c i) -> p c j i", i=LINE),
                )
            for c0, c1 in ((0, middle), (middle, last_quarter), (last_quarter, T)):
                nc.vector.quantize_mx(
                    out=x_words[g][:, c0:c1].bitcast(FP8X4),
                    scales=x_scales[SCALE_ROWS * g : P, c0:c1],
                    in_=rounded[:, c0 * PACK : c1 * PACK],
                )

        def pick(picked, table):
            nc.vector.tensor_copy(picked[:], table[:].indirect(offsets[:]))

        picked_words = {}

        def pick_words(g, tag):
            picked_words[g] = keep.tile([P, S], U32, name="picked_words%d" % g, tag=tag, align_bytes=64)
            pick(picked_words[g], x_words[g])

        w_rounded, w_words, w_scales = {}, {}, {}

        def round_weights(mat, g):
            vector_cols = VECTOR_COLS[mat, g]
            dealt = w_raw[mat, g][:].rearrange("p j (m t) -> p m j t", t=PACK)
            for pair in range(PAIRS):
                name = "w_bf%d%d%d" % (mat, g, pair)
                rounded = keep.tile([P, 2, P, PACK], BF16, name=name, tag=name, align_bytes=64)
                w_rounded[mat, g, pair] = rounded
                lo = min(max(vector_cols.start - pair * P, 0), P)
                hi = min(max(vector_cols.stop - pair * P, 0), P)
                for round_on, m0, m1 in ((round_on_scalar, 0, lo), (round_on_vector, lo, hi), (round_on_scalar, hi, P)):
                    if m1 > m0:
                        round_on(
                            rounded[:, :, m0:m1, :].rearrange("p u m j -> p m j u"),
                            dealt[:, m0:m1, :, 2 * pair : 2 * pair + 2],
                        )

        def quantise_weights(mat, g, spans):
            if (mat, g) not in w_words:
                w_words[mat, g] = keep.tile([P, H], U32, name="w_words%d%d" % (mat, g), align_bytes=64)
                w_scales[mat, g] = keep.tile([P, H], U8, name="w_scales%d%d" % (mat, g), align_bytes=64)
            words, scales = w_words[mat, g], w_scales[mat, g]
            for first, last in spans:
                cols = slice(first, last)
                pair, start = divmod(first, 2 * P)
                rounded = w_rounded[mat, g, pair][:].rearrange("p u m j -> p (u m j)")
                nc.vector.quantize_mx(
                    out=words[:, cols].bitcast(FP8X4),
                    scales=scales[:, cols],
                    in_=rounded[:, start * PACK : (start + last - first) * PACK],
                )

        by_pairs = [(2 * P * pair, 2 * P * (pair + 1)) for pair in range(PAIRS)]
        quantise_tokens(0)
        pick_words(0, "picked_words0")
        quantise_tokens(1)
        round_weights(W1, 0)
        pick(picked_scales, x_scales)
        quantise_weights(W1, 0, by_pairs[:1])
        pick_words(1, "w_raw%d%d" % (W1, 0))

        def first_layer_pass(acc, mat, g, t, tokens, start, stop):
            cols = slice(t * P, (t + 1) * P)
            nc.tensor.matmul_mx(
                out=acc,
                lhsT=w_words[mat, g][:, cols].bitcast(FP8X4),
                lhsT_scale=w_scales[mat, g][:, cols],
                rhs=picked_words[g][:, tokens].bitcast(FP8X4),
                rhs_scale=picked_scales[SCALE_ROWS * g : P, tokens],
                start=start,
                stop=stop,
            )

        quantise_weights(W1, 0, by_pairs[1:])
        w1_banks = {}
        for half in range(2):
            for pair in range(PAIRS):
                name = "w1_bank%d" % (PAIRS * half + pair)
                w1_banks[half, pair] = psum.tile([P, 2, S // 2], F32, name=name, tag=name)

        def w1_pass(half, pair, u, g):
            tokens = slice(half * S // 2, (half + 1) * S // 2)
            start, stop = (g, u) == (0, 0), (g, u) == (PASSES - 1, 1)
            first_layer_pass(w1_banks[half, pair][:, u, :], W1, g, 2 * pair + u, tokens, start, stop)

        for pair in range(PAIRS):
            for u in range(2):
                for half in range(2):
                    w1_pass(half, pair, u, 0)
        round_weights(W1, 1)
        quantise_weights(W1, 1, by_pairs)
        for half in range(2):
            for pair in range(PAIRS):
                for u in range(2):
                    w1_pass(half, pair, u, 1)

        round_weights(W3, 0)
        quantise_weights(W3, 0, by_pairs)
        silu_w1 = {}

        def silu(c, values):
            silu_w1[c] = values
            for pair in range(PAIRS):
                sums = w1_banks[c // 2, pair][:, :, chunk_cols(c % 2, c % 2 + 1)]
                nc.scalar.activation(
                    values[:, :, 2 * pair : 2 * pair + 2, :], sums.rearrange("p u (c i) -> p c u i", i=2), ACT.Silu
                )

        silu(0, keep.tile([P, CHUNK // 2, PACK, 2], F32, name="silu_first", tag="w_raw%d%d" % (W3, 0), align_bytes=64)[:])
        round_weights(W3, 1)
        halves = [(t * P + lo, t * P + lo + P // 2) for lo in (0, P // 2) for t in (2, 3)]
        quantise_weights(W3, 1, by_pairs[:1] + halves)

        last_raw = "w_raw%d%d" % (W3, PASSES - 1)
        silu_rest = keep.tile([P, CHUNKS - 1, CHUNK // 2, PACK, 2], F32, name="silu_rest", tag=last_raw, align_bytes=64)
        for c in range(1, CHUNKS):
            silu(c, silu_rest[:, c - 1, :, :, :])

        w3_banks = [psum.tile([P, PACK, CHUNK], F32, name="w3_bank%d" % c, tag="w3_bank%d" % c) for c in range(CHUNKS)]

        forward = [(t, g) for g in range(PASSES) for t in range(PACK)]
        backward = forward[::-1]
        orders = [forward] + [forward[:PACK] + backward[:PACK]] * (CHUNKS - 1)

        def w3_passes(c, steps):
            for t, g in steps:
                start, stop = (t, g) == orders[c][0], (t, g) == orders[c][-1]
                first_layer_pass(w3_banks[c][:, t, :], W3, g, t, chunk_cols(c, c + 1), start, stop)

        for c in range(CHUNKS):
            w3_passes(c, orders[c][:PACK])
        for c in range(CHUNKS):
            w3_passes(c, orders[c][PACK:])

        results = keep.tile([P, S], F32, name="results")
        hidden = {}
        h_words, h_scales, y_banks = {}, {}, {}

        def held_tile(shape, dtype, name, offset):
            if offset is None:
                return keep.tile(shape, dtype, name=name, align_bytes=64)
            return held.tile(shape, dtype, name=name, align_bytes=64, offset=offset)

        def new_block(k, block, offset=None, scale_tag=None):
            tokens = min(PIECES[k + 1] - PIECES[k] - block * CHUNK, CHUNK)
            name = "%d_%d" % (k, block)
            words = held_tile([P, CHUNK], I32, "h_words" + name, offset)
            tag = scale_tag or "h_scales" + name
            scales = keep.tile([P, CHUNK], U8, name="h_scales" + name, tag=tag, align_bytes=64)
            h_words[k, block], h_scales[k, block] = words, scales
            if tokens < CHUNK:
                nc.vector.memset(words[:, tokens:CHUNK], 0)
                nc.vector.memset(scales[:, tokens:CHUNK].bitcast(I32), 0)

        def new_hidden(first, end, offset=None):
            hidden[first] = (end, held_tile([P, end - first, PACK], BF16, "hidden%d" % first, offset))

        def hidden_cols(first, end):
            start = max(s for s in hidden if s <= first)
            return hidden[start][1][:, first - start : end - start, :]

        def gated_product(first, end):
            c, lo, hi = first // CHUNK, first % CHUNK, (end - 1) % CHUNK + 1
            nc.vector.tensor_tensor(
                hidden_cols(first, end).rearrange("p (c i) t -> p c t i", i=2),
                w3_banks[c][:, :, lo:hi].rearrange("p t (c i) -> p c t i", i=2),
                silu_w1[c][:, lo // 2 : hi // 2, :, :],
                MULT,
            )

        def quantise_hidden(first, end):
            k = max(i for i in range(len(PIECES) - 1) if PIECES[i] <= first)
            block, start = divmod(first - PIECES[k], CHUNK)
            cols = slice(start, start + end - first)
            nc.vector.quantize_mx(
                out=h_words[k, block][:, cols].bitcast(FP8X4),
                scales=h_scales[k, block][:, cols],
                in_=hidden_cols(first, end).rearrange("p c t -> p (c t)"),
            )

        def second_layer(k, block):
            if block == 0:
                width = -(-(PIECES[k + 1] - PIECES[k]) // CHUNK) * CHUNK
                y_banks[k] = psum.tile([P, width], F32, name="y_bank%d" % k, tag="w1_bank%d" % k)
            cols = chunk_cols(block, block + 1)
            nc.tensor.matmul_mx(
                out=y_banks[k][:, cols],
                lhsT=w2_codes[:].bitcast(FP4X4),
                lhsT_scale=w2_plane[:],
                rhs=h_words[k, block][:].bitcast(FP8X4),
                rhs_scale=h_scales[k, block][:],
                start=True,
                stop=True,
            )

        def put(k):
            first, end = PIECES[k], PIECES[k + 1]
            nc.vector.tensor_tensor(results[:, first:end], y_banks[k][:, 0 : end - first], gates[:, first:end], MULT)
            nc.scalar.activation(
                window[:].indirect(places[:, first // LIST_ROWS : end // LIST_ROWS]), results[:, first:end], ACT.Copy
            )

        new_block(0, 0, offset=256)
        new_block(1, 0)
        new_block(1, 1)
        new_block(2, 0)
        new_block(2, 1)
        new_hidden(0, 128)
        gated_product(0, 128)
        new_hidden(128, 256)
        gated_product(128, 192)
        quantise_hidden(0, 128)
        second_layer(0, 0)
        gated_product(192, 256)
        new_hidden(256, 320)
        gated_product(256, 320)
        quantise_hidden(128, 256)
        second_layer(1, 0)
        put(0)
        quantise_hidden(256, 320)
        second_layer(1, 1)
        new_hidden(320, 512, offset=0)
        gated_product(320, 384)
        gated_product(384, 480)
        put(1)
        gated_product(480, 512)
        quantise_hidden(320, 448)
        second_layer(2, 0)
        quantise_hidden(448, 512)
        second_layer(2, 1)
        put(2)

        nc.sync.dma_start(out, window[:])
